import numpy as np
import ml_dtypes


def mxq(x, axis, fmt="e4m3"):
    dtype, down = {"e4m3": (ml_dtypes.float8_e4m3fn, 7), "e5m2": (ml_dtypes.float8_e5m2, 14)}[fmt]
    v = np.moveaxis(np.asarray(x, np.float32).astype(ml_dtypes.bfloat16).astype(np.float64), axis, -1)
    blocks = v.reshape(v.shape[:-1] + (-1, 32))
    amax = np.abs(blocks).max(-1, keepdims=True)
    byte = np.maximum(np.where(amax > 0, np.frexp(amax)[1] - 1 + 127, 0) - down, 1)
    scale = np.exp2(byte - 127.0)
    codes = (blocks / scale).astype(np.float32).astype(dtype).astype(np.float64)
    return np.moveaxis((codes * scale).reshape(v.shape), -1, axis)


WIDE = False


def mx_kscale(k):
    if not WIDE:
        return np.ones(k)
    levels = np.array([10, -10, 5, -5, 0])
    if k % 512:
        return np.exp2(np.random.permutation(np.resize(levels, k // 32))).repeat(32)
    a = np.empty((k // 512, 16))
    for p in range(k // 512):
        a[p, :8] = np.random.permutation(np.resize(levels, 8))
        for g in range(8):
            far = levels[np.abs(levels - a[p, g]) >= 10]
            a[p, g + 8] = far[np.random.randint(len(far))]
    return np.exp2(a.ravel()).repeat(32)


def f64(x):
    return np.asarray(x).astype(np.float64)


def striped(idx):
    return np.tile(idx.reshape(-1, 16).T, (8, 1)).astype(np.uint16)


def unstriped(offs):
    return offs[:16].T.reshape(-1).astype(np.int64)


E2M1 = np.array([0.0, 0.5, 1.0, 1.5, 2.0, 3.0, 4.0, 6.0, -0.0, -0.5, -1.0, -1.5, -2.0, -3.0, -4.0, -6.0])


def pack_weight(w, fmt):
    k, n = w.shape
    w = f64(np.asarray(w, np.float32).astype(ml_dtypes.bfloat16)).reshape(k // 32, 32, n)
    amax = np.abs(w).max(1)
    if fmt == "e4m3":
        byte = np.frexp(amax)[1] - 1 + 127 - 7
    else:
        mant, ex = np.frexp(amax / 6.0)
        byte = np.where(mant > 0.5, ex, ex - 1) + 127
    byte = np.clip(np.where(amax > 0, byte, 1), 1, 254)
    scaled = (w * np.exp2(127.0 - byte)[:, None, :]).reshape(k, n).astype(np.float32)
    by_word = np.ascontiguousarray(scaled.reshape(k // 512, 128, 4, n).transpose(0, 1, 3, 2))
    if fmt == "e4m3":
        words = by_word.astype(ml_dtypes.float8_e4m3fn).view(np.uint8)
    else:
        c = by_word.astype(ml_dtypes.float4_e2m1fn).view(np.uint8) & 0xF
        words = (c[..., 0::2] | (c[..., 1::2] << 4)).reshape(k // 512, 128, 2 * n)
    return np.ascontiguousarray(words), np.ascontiguousarray(byte.astype(np.uint8).reshape(k // 512, 16, n))


def unpack_weight(words, scales, fmt):
    g, _, n = scales.shape
    words = np.ascontiguousarray(words).reshape(g, 128, n, -1)
    if fmt == "e4m3":
        vals = words.view(ml_dtypes.float8_e4m3fn).astype(np.float64)
    else:
        nib = np.empty((g, 128, n, 4), np.uint8)
        nib[..., 0::2] = words & 0xF
        nib[..., 1::2] = words >> 4
        vals = E2M1[nib]
    vals = vals * np.repeat(np.exp2(scales.astype(np.float64) - 127.0), 8, axis=1)[..., None]
    return vals.transpose(0, 1, 3, 2).reshape(g * 512, n)


def relu2(v):
    return np.maximum(v, 0.0) ** 2


K, T, E, C, H, N = 1024, 1024, 16, 128, 512, 256


def by_expert(wq, xq):
    return np.concatenate([wq[e].T @ xq[:, e * C:(e + 1) * C] for e in range(E)], axis=1)


def setup_inputs():
    n = np.random.standard_normal
    s = mx_kscale(K)
    u = mx_kscale(H)
    first = np.random.permutation(np.repeat(np.arange(E), T // E))
    second = (first + 1 + np.random.permutation(np.repeat(np.arange(E - 1), -(-T // (E - 1)))[:T])) % E
    while np.bincount(second, minlength=E).max() != T // E:
        load = np.bincount(second, minlength=E); hi, lo = int(load.argmax()), int(load.argmin())
        t = np.flatnonzero((second == hi) & (first != lo))[0]; second[t] = lo
    slot_token = np.empty(E * C, np.int64); pos = np.empty((2, T), np.int64); fill = np.zeros(E, np.int64)
    place = np.stack([np.random.permutation(C) for _ in range(E)])
    for r, deal in enumerate((first, second)):
        for t in np.random.permutation(T):
            e = deal[t]; j = e * C + place[e, fill[e]]; fill[e] += 1; slot_token[j] = t; pos[r, t] = j
    g = np.random.uniform(0.2, 0.8, T)
    x = pack_weight(n((K, T)) * s[:, None], "e4m3")
    w2 = [pack_weight(m, "e2m1") for m in n((E, H, N)) / np.sqrt(H) / u[None, :, None] ** 2]
    return {
        "x_words": x[0],
        "x_scales": x[1],
        "w1": (n((K, H)) / np.sqrt(K) / s[:, None] * u).astype(np.float32),
        "w2_words": np.stack([m[0] for m in w2]),
        "w2_scales": np.stack([m[1] for m in w2]),
        "gate": np.stack([np.tile(g, (128, 1)), np.tile(1.0 - g, (128, 1))]).astype(np.float32),
        "offs": striped(slot_token),
        "pos1": striped(pos[0]),
        "pos2": striped(pos[1]),
    }


def reference(x_words, x_scales, w1, w2_words, w2_scales, gate, offs, pos1, pos2):
    w1q = mxq(f64(w1), 0, "e4m3")
    w2 = np.stack([unpack_weight(w2_words[e], w2_scales[e], "e2m1") for e in range(E)])
    idx = unstriped(offs)
    x = unpack_weight(x_words, x_scales, "e4m3")
    h = relu2(w1q.T @ x)
    y = by_expert(w2, mxq(h[:, idx], 0, "e4m3"))
    out = sum(f64(gate[r, :1]) * y[:, unstriped(p)] for r, p in enumerate((pos1, pos2)))
    return out

@@ -1,0 +1,218 @@
+from contextlib import ExitStack
+
+import concourse.mybir as mybir
+
+K, T, E, C, H, N = 1024, 1024, 16, 128, 512, 256
+S = E * C
+FLOPS = 2 * K * H * T + 2 * H * N * S
+
+F32 = mybir.dt.float32
+BF16 = mybir.dt.bfloat16
+I32 = mybir.dt.int32
+U32 = mybir.dt.uint32
+U16 = mybir.dt.uint16
+U8 = mybir.dt.uint8
+FP8X4 = mybir.dt.float8_e4m3fn_x4
+FP4X4 = mybir.dt.float4_e2m1fn_x4
+ACT = mybir.ActivationFunctionType
+ALU = mybir.AluOpType
+
+P = 128
+HALF = T // 2
+FIRST_PAIR_CUTS = (768, 768, 512)
+SLOT_CHUNKS = (256, 512, 512, 256, 256, 256)
+DIRECT_FROM = 2048
+TOKEN_CHUNKS = ((1024,), (512, 256, 256))
+
+
+def spans(widths):
+    out, start = [], 0
+    for w in widths:
+        out.append((start, start + w))
+        start += w
+    return out
+
+
+def tile_moe_sup_lin_relu2_kernel(tc, x_words, x_scales, w1, w2_words, w2_scales, gate, offs, pos1, pos2, out):
+    nc = tc.nc
+    with ExitStack() as ctx:
+        lists = ctx.enter_context(tc.tile_pool(name="lists", bufs=1))
+        keep = ctx.enter_context(tc.tile_pool(name="keep", bufs=1))
+        psum = ctx.enter_context(tc.psum_pool(name="psum", bufs=1))
+
+        x_plane = keep.tile([P, 2, T], U8, name="x_plane", align_bytes=64)
+        nc.vector.memset(x_plane[:].bitcast(I32), 0)
+
+        w1_raw = [keep.tile([P, 4, H], F32, name="w1_raw%d" % s, tag="big%d" % s, align_bytes=64) for s in range(2)]
+        x_first = [keep.tile([P, 4 * HALF], U8, name="x_first%d" % s, align_bytes=64) for s in range(2)]
+        x_second = keep.tile([P, 2, 4 * HALF], U8, name="x_second", align_bytes=64)
+        x_rows = x_words.rearrange("s p t d -> p s (t d)")
+
+        def load_w1(s):
+            nc.sync.dma_start(out=w1_raw[s][:], in_=w1[512 * s : 512 * (s + 1), :].rearrange("(p j) c -> p j c", j=4))
+
+        load_w1(0)
+        x_scale_rows = x_scales.rearrange("s (q r) t -> r q s t", r=4)
+        for r in range(4):
+            nc.gpsimd.dma_start(out=x_plane[r:P:32, :, :].bitcast(I32), in_=x_scale_rows[r].bitcast(I32))
+        nc.sync.dma_start(out=x_first[0][:].bitcast(I32), in_=x_rows[:, 0, : 4 * HALF].bitcast(I32))
+        load_w1(1)
+        nc.sync.dma_start(out=x_first[1][:].bitcast(I32), in_=x_rows[:, 1, : 4 * HALF].bitcast(I32))
+        nc.sync.dma_start(out=x_second[:].bitcast(I32), in_=x_rows[:, :, 4 * HALF :].bitcast(I32))
+        slot_list = lists.tile([P, S // 16], U16, name="slot_list")
+        nc.sync.dma_start(slot_list[:], offs)
+        back_lists = [lists.tile([P, T // 16], U16, name="back_list%d" % r) for r in range(2)]
+        nc.sync.dma_start(back_lists[0][:], pos1)
+        nc.sync.dma_start(back_lists[1][:], pos2)
+
+        def x_codes(s, h):
+            words = x_first[s][:] if h == 0 else x_second[:, s, :]
+            return words.bitcast(FP8X4)
+
+        w1_codes, w1_plane = {}, {}
+
+        def quantise_w1(s):
+            grouped = []
+            for u in range(2):
+                g = keep.tile([P, 2, P, 4], BF16, name="w1_grouped%d%d" % (s, u), tag="grouped%d%d" % (s, u), align_bytes=64)
+                src = w1_raw[s][:].rearrange("p j (m t) -> p m t j", t=4)[:, :, 2 * u : 2 * u + 2, :]
+                dst = g[:].rearrange("p t m j -> p m t j")
+                if u == 0:
+                    nc.vector.tensor_copy(out=dst, in_=src)
+                else:
+                    nc.scalar.activation(out=dst, in_=src, func=ACT.Copy)
+                grouped.append(g)
+            for u in range(2):
+                w1_codes[s, u] = keep.tile([P, 2 * P], U32, name="w1_codes%d%d" % (s, u), align_bytes=64)
+                w1_plane[s, u] = keep.tile([P, 2 * P], U8, name="w1_plane%d%d" % (s, u), align_bytes=64)
+                nc.vector.quantize_mx(
+                    out=w1_codes[s, u][:].bitcast(FP8X4),
+                    scales=w1_plane[s, u][:],
+                    in_=grouped[u][:].rearrange("p t m j -> p (t m j)"),
+                )
+
+        sums = {(t, h): psum.tile([P, HALF], F32, name="sums%d%d" % (t, h), tag="bank%d" % (4 * (t // 2) + 2 * h + t % 2))
+                for t in range(4) for h in range(2)}
+
+        def first_layer(s, t, h):
+            cols = slice(P * (t % 2), P * (t % 2 + 1))
+            nc.tensor.matmul_mx(
+                out=sums[t, h][:],
+                lhsT=w1_codes[s, t // 2][:, cols].bitcast(FP8X4),
+                lhsT_scale=w1_plane[s, t // 2][:, cols],
+                rhs=x_codes(s, h),
+                rhs_scale=x_plane[:, s, HALF * h : HALF * (h + 1)],
+                start=(s == 0),
+                stop=(s == 1),
+            )
+
+        quantise_w1(0)
+        w2_plane = keep.tile([P, E, N], U8, name="w2_plane", tag="grouped00", align_bytes=64)
+        nc.vector.memset(w2_plane[:].bitcast(I32), 0)
+        w2_scale_rows = w2_scales.rearrange("e s (q r) n -> r q (e s) n", r=4)
+        for r in range(4):
+            nc.sync.dma_start(out=w2_plane[r:P:32, :, :].bitcast(I32), in_=w2_scale_rows[r].bitcast(I32))
+        for t in range(2):
+            first_layer(0, t, 0)
+        quantise_w1(1)
+        w2_codes = keep.tile([P, E, 2 * N], U8, name="w2_codes", tag="big0", align_bytes=64)
+        gates = keep.tile([P, 2, T], F32, name="gates", tag="big1", align_bytes=64)
+        w2_rows = w2_words.rearrange("e s p b -> p (e s) b")
+        for e0 in range(0, E, E // 2):
+            nc.sync.dma_start(out=w2_codes[:, e0 : e0 + E // 2, :].bitcast(I32), in_=w2_rows[:, e0 : e0 + E // 2, :].bitcast(I32))
+        nc.sync.dma_start(out=gates[:], in_=gate.rearrange("r p t -> p r t"))
+
+        pairs = [keep.tile([P, T, 2], BF16, name="pairs%d" % u, align_bytes=64) for u in range(2)]
+        for u in range(2):
+            for h in range(2):
+                for t in (2 * u, 2 * u + 1):
+                    if h == 1 or u == 1:
+                        first_layer(0, t, h)
+                    first_layer(1, t, h)
+                pos = keep.tile([P, 2, HALF], F32, name="pos%d%d" % (u, h))
+                nc.scalar.activation(out=pos[:, 0, :], in_=sums[2 * u, h][:], func=ACT.Relu)
+                if u == 0:
+                    nc.vector.tensor_scalar_max(out=pos[:, 1, :], in0=sums[2 * u + 1, h][:], scalar1=0.0)
+                else:
+                    nc.scalar.activation(out=pos[:, 1, :], in_=sums[2 * u + 1, h][:], func=ACT.Relu)
+                by_token = pos[:].rearrange("p e n -> p n e")
+                cut = HALF // 2 if u == 0 else 0
+                if cut:
+                    nc.vector.tensor_tensor(out=pairs[u][:, HALF * h : HALF * h + cut, :], in0=by_token[:, :cut, :],
+                                            in1=by_token[:, :cut, :], op=ALU.mult)
+                nc.scalar.activation(out=pairs[u][:, HALF * h + cut : HALF * (h + 1), :], in_=by_token[:, cut:, :], func=ACT.Square)
+
+        windows = [pairs[u][:].rearrange("p n e -> p (n e)").bitcast(U32) for u in range(2)]
+        slots = keep.tile([P, S, 4], BF16, name="slots", align_bytes=64)
+        slot_words = slots[:].bitcast(U32)
+        picked = keep.tile([P, 2, S, 2], BF16, name="picked", align_bytes=64)
+        picked_words = picked[:].rearrange("p u n e -> p u (n e)").bitcast(U32)
+
+        def gather_pairs(u, a, b):
+            dst = slot_words[:, a:b, u] if a >= DIRECT_FROM else picked_words[:, u, a:b]
+            nc.vector.tensor_copy(out=dst, in_=windows[u].indirect(slot_list[:, a // 16 : b // 16]))
+
+        for a, b in spans(FIRST_PAIR_CUTS):
+            gather_pairs(0, a, b)
+
+        h_codes = keep.tile([P, S], U32, name="h_codes", align_bytes=64)
+        h_plane = keep.tile([P, S], U8, name="h_plane", align_bytes=64)
+        y = [keep.tile([P, S], F32, name="y%d" % r) for r in range(2)]
+
+        def second_layer(rows, a, b, bank, on_vector):
+            acc = psum.tile([P, b - a], F32, name="acc%d_%d" % (rows, a), tag="bank%d" % bank)
+            for e in range(a // C, b // C):
+                nc.tensor.matmul_mx(
+                    out=acc[:, C * e - a : C * (e + 1) - a],
+                    lhsT=w2_codes[:, e, 2 * P * rows : 2 * P * (rows + 1)].bitcast(FP4X4),
+                    lhsT_scale=w2_plane[:, e, P * rows : P * (rows + 1)],
+                    rhs=h_codes[:, C * e : C * (e + 1)].bitcast(FP8X4),
+                    rhs_scale=h_plane[:, C * e : C * (e + 1)],
+                    start=True,
+                    stop=True,
+                )
+            if on_vector:
+                nc.vector.tensor_copy(out=y[rows][:, a:b], in_=acc[:])
+            else:
+                nc.scalar.copy(out=y[rows][:, a:b], in_=acc[:])
+
+        def quantise_slots(i, a, b):
+            nc.vector.quantize_mx(
+                out=h_codes[:, a:b].bitcast(FP8X4),
+                scales=h_plane[:, a:b],
+                in_=slots[:, a:b, :].rearrange("p n d -> p (n d)"),
+            )
+
+        chunks = spans(SLOT_CHUNKS)
+        for i, (a, b) in enumerate(chunks):
+            gather_pairs(1, a, b)
+            if a < DIRECT_FROM:
+                nc.scalar.copy(out=slots[:, a:b, :].rearrange("p n (u e) -> p n u e", u=2),
+                               in_=picked[:, :, a:b, :].rearrange("p u n e -> p n u e"))
+            if i > 0:
+                quantise_slots(i - 1, *chunks[i - 1])
+        quantise_slots(len(chunks) - 1, *chunks[-1])
+        for i, (a, b) in enumerate(chunks):
+            second_layer(0, a, b, i, i == len(chunks) - 1)
+        for i in range(4):
+            second_layer(1, 512 * i, 512 * (i + 1), (len(chunks) + i) % 8, False)
+
+        pieces = [(rows, a, b) for rows in range(2) for a, b in spans(TOKEN_CHUNKS[rows])]
+        terms = {}
+
+        def fetch(rows, a, b):
+            for r in range(2):
+                terms[rows, a, r] = keep.tile([P, b - a], F32, name="term%d_%d_%d" % (rows, a, r))
+                nc.vector.tensor_tensor(out=terms[rows, a, r][:], in0=y[rows][:].indirect(back_lists[r][:, a // 16 : b // 16]),
+                                        in1=gates[:, r, a:b], op=ALU.mult)
+
+        def combine(rows, a, b):
+            res = keep.tile([P, b - a], F32, name="res%d_%d" % (rows, a))
+            nc.vector.tensor_tensor(out=res[:], in0=terms[rows, a, 0][:], in1=terms[rows, a, 1][:], op=ALU.add)
+            nc.sync.dma_start(out=out[P * rows : P * (rows + 1), a:b], in_=res[:])
+
+        for i, piece in enumerate(pieces):
+            fetch(*piece)
+            if i > 0:
+                combine(*pieces[i - 1])
+        combine(*pieces[-1])

@@ -19,18 +19,19 @@ ALU = mybir.AluOpType
 
 P = 128
 HALF = T // 2
+BANK = 512
+W1_CUTS = ((512,), (256, 256))
 FIRST_PAIR_CUTS = (768, 768, 512)
 SLOT_CHUNKS = (256, 512, 512, 256, 256, 256)
-DIRECT_FROM = 2048
 TOKEN_CHUNKS = ((1024,), (512, 256, 256))
 
 
 def spans(widths):
-    out, start = [], 0
-    for w in widths:
-        out.append((start, start + w))
-        start += w
-    return out
+    cuts, start = [], 0
+    for width in widths:
+        cuts.append((start, start + width))
+        start += width
+    return cuts
 
 
 def tile_moe_sup_lin_relu2_kernel(tc, x_words, x_scales, w1, w2_words, w2_scales, gate, offs, pos1, pos2, out):
@@ -44,44 +45,41 @@ def tile_moe_sup_lin_relu2_kernel(tc, x_words, x_scales, w1, w2_words, w2_scales
         nc.vector.memset(x_plane[:].bitcast(I32), 0)
 
         w1_raw = [keep.tile([P, 4, H], F32, name="w1_raw%d" % s, tag="big%d" % s, align_bytes=64) for s in range(2)]
-        x_first = [keep.tile([P, 4 * HALF], U8, name="x_first%d" % s, align_bytes=64) for s in range(2)]
-        x_second = keep.tile([P, 2, 4 * HALF], U8, name="x_second", align_bytes=64)
-        x_rows = x_words.rearrange("s p t d -> p s (t d)")
+        x_pass = [keep.tile([P, 4 * T], U8, name="x_pass%d" % s, align_bytes=64) for s in range(2)]
+        x_rows = x_words.rearrange("s p t d -> s p (t d)")
+        w1_rows = w1.rearrange("(s p j) c -> s p j c", s=2, j=4)
 
         def load_w1(s):
-            nc.sync.dma_start(out=w1_raw[s][:], in_=w1[512 * s : 512 * (s + 1), :].rearrange("(p j) c -> p j c", j=4))
+            for a, b in spans(W1_CUTS[s]):
+                nc.sync.dma_start(out=w1_raw[s][:, :, a:b], in_=w1_rows[s, :, :, a:b])
+
+        def load_x(s, a, b):
+            nc.sync.dma_start(out=x_pass[s][:, 4 * a : 4 * b].bitcast(I32), in_=x_rows[s, :, 4 * a : 4 * b].bitcast(I32))
 
         load_w1(0)
         x_scale_rows = x_scales.rearrange("s (q r) t -> r q s t", r=4)
         for r in range(4):
-            nc.gpsimd.dma_start(out=x_plane[r:P:32, :, :].bitcast(I32), in_=x_scale_rows[r].bitcast(I32))
-        nc.sync.dma_start(out=x_first[0][:].bitcast(I32), in_=x_rows[:, 0, : 4 * HALF].bitcast(I32))
+            nc.scalar.dma_start(out=x_plane[r:P:32, :, :].bitcast(I32), in_=x_scale_rows[r].bitcast(I32))
+        load_x(0, 0, T)
         load_w1(1)
-        nc.sync.dma_start(out=x_first[1][:].bitcast(I32), in_=x_rows[:, 1, : 4 * HALF].bitcast(I32))
-        nc.sync.dma_start(out=x_second[:].bitcast(I32), in_=x_rows[:, :, 4 * HALF :].bitcast(I32))
+        load_x(1, 0, HALF)
+        load_x(1, HALF, T)
         slot_list = lists.tile([P, S // 16], U16, name="slot_list")
         nc.sync.dma_start(slot_list[:], offs)
         back_lists = [lists.tile([P, T // 16], U16, name="back_list%d" % r) for r in range(2)]
         nc.sync.dma_start(back_lists[0][:], pos1)
         nc.sync.dma_start(back_lists[1][:], pos2)
 
-        def x_codes(s, h):
-            words = x_first[s][:] if h == 0 else x_second[:, s, :]
-            return words.bitcast(FP8X4)
-
         w1_codes, w1_plane = {}, {}
 
         def quantise_w1(s):
-            grouped = []
-            for u in range(2):
-                g = keep.tile([P, 2, P, 4], BF16, name="w1_grouped%d%d" % (s, u), tag="grouped%d%d" % (s, u), align_bytes=64)
-                src = w1_raw[s][:].rearrange("p j (m t) -> p m t j", t=4)[:, :, 2 * u : 2 * u + 2, :]
-                dst = g[:].rearrange("p t m j -> p m t j")
-                if u == 0:
-                    nc.vector.tensor_copy(out=dst, in_=src)
-                else:
-                    nc.scalar.activation(out=dst, in_=src, func=ACT.Copy)
-                grouped.append(g)
+            grouped = [keep.tile([P, 2, P, 4], BF16, name="w1_grouped%d%d" % (s, u), tag="grouped%d%d" % (s, u), align_bytes=64)
+                       for u in range(2)]
+            by_channel = w1_raw[s][:].rearrange("p j (m t) -> p m t j", t=4)
+            for a, b in spans(W1_CUTS[s]):
+                ms = slice(a // 4, b // 4)
+                nc.vector.tensor_copy(out=grouped[0][:].rearrange("p t m j -> p m t j")[:, ms], in_=by_channel[:, ms, 0:2, :])
+                nc.scalar.activation(out=grouped[1][:].rearrange("p t m j -> p m t j")[:, ms], in_=by_channel[:, ms, 2:4, :], func=ACT.Copy)
             for u in range(2):
                 w1_codes[s, u] = keep.tile([P, 2 * P], U32, name="w1_codes%d%d" % (s, u), align_bytes=64)
                 w1_plane[s, u] = keep.tile([P, 2 * P], U8, name="w1_plane%d%d" % (s, u), align_bytes=64)
@@ -100,7 +98,7 @@ def tile_moe_sup_lin_relu2_kernel(tc, x_words, x_scales, w1, w2_words, w2_scales
                 out=sums[t, h][:],
                 lhsT=w1_codes[s, t // 2][:, cols].bitcast(FP8X4),
                 lhsT_scale=w1_plane[s, t // 2][:, cols],
-                rhs=x_codes(s, h),
+                rhs=x_pass[s][:, 4 * HALF * h : 4 * HALF * (h + 1)].bitcast(FP8X4),
                 rhs_scale=x_plane[:, s, HALF * h : HALF * (h + 1)],
                 start=(s == 0),
                 stop=(s == 1),
@@ -112,30 +110,28 @@ def tile_moe_sup_lin_relu2_kernel(tc, x_words, x_scales, w1, w2_words, w2_scales
         w2_scale_rows = w2_scales.rearrange("e s (q r) n -> r q (e s) n", r=4)
         for r in range(4):
             nc.sync.dma_start(out=w2_plane[r:P:32, :, :].bitcast(I32), in_=w2_scale_rows[r].bitcast(I32))
-        for t in range(2):
-            first_layer(0, t, 0)
+        for u in range(2):
+            for h in range(2):
+                for t in (2 * u, 2 * u + 1):
+                    first_layer(0, t, h)
         quantise_w1(1)
         w2_codes = keep.tile([P, E, 2 * N], U8, name="w2_codes", tag="big0", align_bytes=64)
         gates = keep.tile([P, 2, T], F32, name="gates", tag="big1", align_bytes=64)
-        w2_rows = w2_words.rearrange("e s p b -> p (e s) b")
-        for e0 in range(0, E, E // 2):
-            nc.sync.dma_start(out=w2_codes[:, e0 : e0 + E // 2, :].bitcast(I32), in_=w2_rows[:, e0 : e0 + E // 2, :].bitcast(I32))
+        nc.sync.dma_start(out=w2_codes[:].bitcast(I32), in_=w2_words.rearrange("e s p b -> p (e s) b").bitcast(I32))
         nc.sync.dma_start(out=gates[:], in_=gate.rearrange("r p t -> p r t"))
 
         pairs = [keep.tile([P, T, 2], BF16, name="pairs%d" % u, align_bytes=64) for u in range(2)]
         for u in range(2):
             for h in range(2):
                 for t in (2 * u, 2 * u + 1):
-                    if h == 1 or u == 1:
-                        first_layer(0, t, h)
                     first_layer(1, t, h)
-                pos = keep.tile([P, 2, HALF], F32, name="pos%d%d" % (u, h))
-                nc.scalar.activation(out=pos[:, 0, :], in_=sums[2 * u, h][:], func=ACT.Relu)
+                positive = keep.tile([P, 2, HALF], F32, name="positive%d%d" % (u, h))
+                nc.scalar.activation(out=positive[:, 0, :], in_=sums[2 * u, h][:], func=ACT.Relu)
                 if u == 0:
-                    nc.vector.tensor_scalar_max(out=pos[:, 1, :], in0=sums[2 * u + 1, h][:], scalar1=0.0)
+                    nc.vector.tensor_scalar_max(out=positive[:, 1, :], in0=sums[2 * u + 1, h][:], scalar1=0.0)
                 else:
-                    nc.scalar.activation(out=pos[:, 1, :], in_=sums[2 * u + 1, h][:], func=ACT.Relu)
-                by_token = pos[:].rearrange("p e n -> p n e")
+                    nc.scalar.activation(out=positive[:, 1, :], in_=sums[2 * u + 1, h][:], func=ACT.Relu)
+                by_token = positive[:].rearrange("p e n -> p n e")
                 cut = HALF // 2 if u == 0 else 0
                 if cut:
                     nc.vector.tensor_tensor(out=pairs[u][:, HALF * h : HALF * h + cut, :], in0=by_token[:, :cut, :],
@@ -143,23 +139,18 @@ def tile_moe_sup_lin_relu2_kernel(tc, x_words, x_scales, w1, w2_words, w2_scales
                 nc.scalar.activation(out=pairs[u][:, HALF * h + cut : HALF * (h + 1), :], in_=by_token[:, cut:, :], func=ACT.Square)
 
         windows = [pairs[u][:].rearrange("p n e -> p (n e)").bitcast(U32) for u in range(2)]
-        slots = keep.tile([P, S, 4], BF16, name="slots", align_bytes=64)
-        slot_words = slots[:].bitcast(U32)
         picked = keep.tile([P, 2, S, 2], BF16, name="picked", align_bytes=64)
         picked_words = picked[:].rearrange("p u n e -> p u (n e)").bitcast(U32)
-
-        def gather_pairs(u, a, b):
-            dst = slot_words[:, a:b, u] if a >= DIRECT_FROM else picked_words[:, u, a:b]
-            nc.vector.tensor_copy(out=dst, in_=windows[u].indirect(slot_list[:, a // 16 : b // 16]))
-
-        for a, b in spans(FIRST_PAIR_CUTS):
-            gather_pairs(0, a, b)
-
+        slots = keep.tile([P, S, 4], BF16, name="slots", align_bytes=64)
+        slot_words = slots[:].bitcast(U32)
         h_codes = keep.tile([P, S], U32, name="h_codes", align_bytes=64)
         h_plane = keep.tile([P, S], U8, name="h_plane", align_bytes=64)
         y = [keep.tile([P, S], F32, name="y%d" % r) for r in range(2)]
 
-        def second_layer(rows, a, b, bank, on_vector):
+        def gather_pairs(u, a, b):
+            nc.vector.tensor_copy(out=picked_words[:, u, a:b], in_=windows[u].indirect(slot_list[:, a // 16 : b // 16]))
+
+        def second_layer(rows, a, b, bank):
             acc = psum.tile([P, b - a], F32, name="acc%d_%d" % (rows, a), tag="bank%d" % bank)
             for e in range(a // C, b // C):
                 nc.tensor.matmul_mx(
@@ -171,31 +162,29 @@ def tile_moe_sup_lin_relu2_kernel(tc, x_words, x_scales, w1, w2_words, w2_scales
                     start=True,
                     stop=True,
                 )
-            if on_vector:
-                nc.vector.tensor_copy(out=y[rows][:, a:b], in_=acc[:])
-            else:
-                nc.scalar.copy(out=y[rows][:, a:b], in_=acc[:])
+            return acc
 
-        def quantise_slots(i, a, b):
+        for a, b in spans(FIRST_PAIR_CUTS):
+            gather_pairs(0, a, b)
+        chunks = spans(SLOT_CHUNKS)
+        first_rows = []
+        for i, (a, b) in enumerate(chunks):
+            gather_pairs(1, a, b)
+            nc.scalar.copy(out=slot_words[:, a:b, :], in_=picked_words[:, :, a:b].rearrange("p u n -> p n u"))
             nc.vector.quantize_mx(
                 out=h_codes[:, a:b].bitcast(FP8X4),
                 scales=h_plane[:, a:b],
                 in_=slots[:, a:b, :].rearrange("p n d -> p (n d)"),
             )
-
-        chunks = spans(SLOT_CHUNKS)
+            first_rows.append(second_layer(0, a, b, i))
+        last = len(chunks) - 1
         for i, (a, b) in enumerate(chunks):
-            gather_pairs(1, a, b)
-            if a < DIRECT_FROM:
-                nc.scalar.copy(out=slots[:, a:b, :].rearrange("p n (u e) -> p n u e", u=2),
-                               in_=picked[:, :, a:b, :].rearrange("p u n e -> p n u e"))
-            if i > 0:
-                quantise_slots(i - 1, *chunks[i - 1])
-        quantise_slots(len(chunks) - 1, *chunks[-1])
-        for i, (a, b) in enumerate(chunks):
-            second_layer(0, a, b, i, i == len(chunks) - 1)
-        for i in range(4):
-            second_layer(1, 512 * i, 512 * (i + 1), (len(chunks) + i) % 8, False)
+            if i == last:
+                nc.vector.tensor_copy(out=y[0][:, a:b], in_=first_rows[i][:])
+            else:
+                nc.scalar.copy(out=y[0][:, a:b], in_=first_rows[i][:])
+        for i, (a, b) in enumerate(spans((BANK,) * (S // BANK))):
+            nc.scalar.copy(out=y[1][:, a:b], in_=second_layer(1, a, b, last - i % 2)[:])
 
         pieces = [(rows, a, b) for rows in range(2) for a, b in spans(TOKEN_CHUNKS[rows])]
         terms = {}

@@ -22,8 +22,9 @@ HALF = T // 2
 BANK = 512
 W1_CUTS = ((512,), (256, 256))
 FIRST_PAIR_CUTS = (768, 768, 512)
-SLOT_CHUNKS = (256, 512, 512, 256, 256, 256)
-TOKEN_CHUNKS = ((1024,), (512, 256, 256))
+SECOND_PAIR_CUTS = (256,) * 8
+SLOT_CHUNKS = (256,) * 7 + (128, 128)
+TOKEN_CHUNKS = ((1024,), (512, 384, 128))
 
 
 def spans(widths):
@@ -83,11 +84,12 @@ def tile_moe_sup_lin_relu2_kernel(tc, x_words, x_scales, w1, w2_words, w2_scales
             for u in range(2):
                 w1_codes[s, u] = keep.tile([P, 2 * P], U32, name="w1_codes%d%d" % (s, u), align_bytes=64)
                 w1_plane[s, u] = keep.tile([P, 2 * P], U8, name="w1_plane%d%d" % (s, u), align_bytes=64)
-                nc.vector.quantize_mx(
-                    out=w1_codes[s, u][:].bitcast(FP8X4),
-                    scales=w1_plane[s, u][:],
-                    in_=grouped[u][:].rearrange("p t m j -> p (t m j)"),
-                )
+                for a, b in spans((1, 1) if (s, u) == (1, 0) else (2,)):
+                    nc.vector.quantize_mx(
+                        out=w1_codes[s, u][:, P * a : P * b].bitcast(FP8X4),
+                        scales=w1_plane[s, u][:, P * a : P * b],
+                        in_=grouped[u][:, a:b].rearrange("p t m j -> p (t m j)"),
+                    )
 
         sums = {(t, h): psum.tile([P, HALF], F32, name="sums%d%d" % (t, h), tag="bank%d" % (4 * (t // 2) + 2 * h + t % 2))
                 for t in range(4) for h in range(2)}
@@ -110,10 +112,9 @@ def tile_moe_sup_lin_relu2_kernel(tc, x_words, x_scales, w1, w2_words, w2_scales
         w2_scale_rows = w2_scales.rearrange("e s (q r) n -> r q (e s) n", r=4)
         for r in range(4):
             nc.sync.dma_start(out=w2_plane[r:P:32, :, :].bitcast(I32), in_=w2_scale_rows[r].bitcast(I32))
-        for u in range(2):
+        for t in range(4):
             for h in range(2):
-                for t in (2 * u, 2 * u + 1):
-                    first_layer(0, t, h)
+                first_layer(0, t, h)
         quantise_w1(1)
         w2_codes = keep.tile([P, E, 2 * N], U8, name="w2_codes", tag="big0", align_bytes=64)
         gates = keep.tile([P, 2, T], F32, name="gates", tag="big1", align_bytes=64)
@@ -121,22 +122,32 @@ def tile_moe_sup_lin_relu2_kernel(tc, x_words, x_scales, w1, w2_words, w2_scales
         nc.sync.dma_start(out=gates[:], in_=gate.rearrange("r p t -> p r t"))
 
         pairs = [keep.tile([P, T, 2], BF16, name="pairs%d" % u, align_bytes=64) for u in range(2)]
+
+        def relu(on_vector, dst, src):
+            if on_vector:
+                nc.vector.tensor_scalar_max(out=dst, in0=src, scalar1=0.0)
+            else:
+                nc.scalar.activation(out=dst, in_=src, func=ACT.Relu)
+
+        def square(on_vector, dst, src):
+            if on_vector:
+                nc.vector.tensor_tensor(out=dst, in0=src, in1=src, op=ALU.mult)
+            else:
+                nc.scalar.activation(out=dst, in_=src, func=ACT.Square)
+
         for u in range(2):
-            for h in range(2):
-                for t in (2 * u, 2 * u + 1):
+            for t in (2 * u, 2 * u + 1):
+                for h in range(2):
                     first_layer(1, t, h)
+            for h in range(2):
+                on_vector = (u, h) == (0, 1)
                 positive = keep.tile([P, 2, HALF], F32, name="positive%d%d" % (u, h))
-                nc.scalar.activation(out=positive[:, 0, :], in_=sums[2 * u, h][:], func=ACT.Relu)
-                if u == 0:
-                    nc.vector.tensor_scalar_max(out=positive[:, 1, :], in0=sums[2 * u + 1, h][:], scalar1=0.0)
-                else:
-                    nc.scalar.activation(out=positive[:, 1, :], in_=sums[2 * u + 1, h][:], func=ACT.Relu)
-                by_token = positive[:].rearrange("p e n -> p n e")
-                cut = HALF // 2 if u == 0 else 0
-                if cut:
-                    nc.vector.tensor_tensor(out=pairs[u][:, HALF * h : HALF * h + cut, :], in0=by_token[:, :cut, :],
-                                            in1=by_token[:, :cut, :], op=ALU.mult)
-                nc.scalar.activation(out=pairs[u][:, HALF * h + cut : HALF * (h + 1), :], in_=by_token[:, cut:, :], func=ACT.Square)
+                relu(on_vector, positive[:, 0, :], sums[2 * u, h][:])
+                quarters = spans((HALF // 2, HALF // 2) if u == 0 else (HALF,))
+                for a, b in quarters:
+                    relu(on_vector, positive[:, 1, a:b], sums[2 * u + 1, h][:, a:b])
+                for a, b in quarters:
+                    square(on_vector, pairs[u][:, HALF * h + a : HALF * h + b, :], positive[:, :, a:b].rearrange("p e n -> p n e"))
 
         windows = [pairs[u][:].rearrange("p n e -> p (n e)").bitcast(U32) for u in range(2)]
         picked = keep.tile([P, 2, S, 2], BF16, name="picked", align_bytes=64)
@@ -166,42 +177,43 @@ def tile_moe_sup_lin_relu2_kernel(tc, x_words, x_scales, w1, w2_words, w2_scales
 
         for a, b in spans(FIRST_PAIR_CUTS):
             gather_pairs(0, a, b)
+        for a, b in spans(SECOND_PAIR_CUTS):
+            gather_pairs(1, a, b)
+            nc.scalar.copy(out=slot_words[:, a:b, :], in_=picked_words[:, :, a:b].rearrange("p u n -> p n u"))
         chunks = spans(SLOT_CHUNKS)
         first_rows = []
         for i, (a, b) in enumerate(chunks):
-            gather_pairs(1, a, b)
-            nc.scalar.copy(out=slot_words[:, a:b, :], in_=picked_words[:, :, a:b].rearrange("p u n -> p n u"))
             nc.vector.quantize_mx(
                 out=h_codes[:, a:b].bitcast(FP8X4),
                 scales=h_plane[:, a:b],
                 in_=slots[:, a:b, :].rearrange("p n d -> p (n d)"),
             )
-            first_rows.append(second_layer(0, a, b, i))
+            first_rows.append(second_layer(0, a, b, i % 8))
         last = len(chunks) - 1
         for i, (a, b) in enumerate(chunks):
-            if i == last:
+            if i >= last - 1:
                 nc.vector.tensor_copy(out=y[0][:, a:b], in_=first_rows[i][:])
             else:
                 nc.scalar.copy(out=y[0][:, a:b], in_=first_rows[i][:])
         for i, (a, b) in enumerate(spans((BANK,) * (S // BANK))):
-            nc.scalar.copy(out=y[1][:, a:b], in_=second_layer(1, a, b, last - i % 2)[:])
+            nc.scalar.copy(out=y[1][:, a:b], in_=second_layer(1, a, b, (last - i % 2) % 8)[:])
 
         pieces = [(rows, a, b) for rows in range(2) for a, b in spans(TOKEN_CHUNKS[rows])]
         terms = {}
 
-        def fetch(rows, a, b):
-            for r in range(2):
-                terms[rows, a, r] = keep.tile([P, b - a], F32, name="term%d_%d_%d" % (rows, a, r))
-                nc.vector.tensor_tensor(out=terms[rows, a, r][:], in0=y[rows][:].indirect(back_lists[r][:, a // 16 : b // 16]),
-                                        in1=gates[:, r, a:b], op=ALU.mult)
+        def fetch(r, rows, a, b):
+            terms[rows, a, r] = keep.tile([P, b - a], F32, name="term%d_%d_%d" % (rows, a, r))
+            nc.vector.tensor_tensor(out=terms[rows, a, r][:], in0=y[rows][:].indirect(back_lists[r][:, a // 16 : b // 16]),
+                                    in1=gates[:, r, a:b], op=ALU.mult)
 
-        def combine(rows, a, b):
+        def combine(queue, rows, a, b):
             res = keep.tile([P, b - a], F32, name="res%d_%d" % (rows, a))
             nc.vector.tensor_tensor(out=res[:], in0=terms[rows, a, 0][:], in1=terms[rows, a, 1][:], op=ALU.add)
-            nc.sync.dma_start(out=out[P * rows : P * (rows + 1), a:b], in_=res[:])
+            queue.dma_start(out=out[P * rows : P * (rows + 1), a:b], in_=res[:])
 
         for i, piece in enumerate(pieces):
-            fetch(*piece)
+            fetch(0, *piece)
             if i > 0:
-                combine(*pieces[i - 1])
-        combine(*pieces[-1])
+                combine(nc.sync, *pieces[i - 1])
+            fetch(1, *piece)
+        combine(nc.scalar, *pieces[-1])

@@ -1,6 +1,7 @@
 from contextlib import ExitStack
 
 import concourse.mybir as mybir
+from concourse.masks import make_identity
 
 K, T, E, C, H, N = 1024, 1024, 16, 128, 512, 256
 S = E * C
@@ -24,7 +25,8 @@ W1_CUTS = ((512,), (256, 256))
 FIRST_PAIR_CUTS = (768, 768, 512)
 SECOND_PAIR_CUTS = (256,) * 8
 SLOT_CHUNKS = (256,) * 7 + (128, 128)
-TOKEN_CHUNKS = ((1024,), (512, 384, 128))
+PSUM_PIECES = 2
+TOKEN_CHUNKS = ((512, 512), (512, 384, 128))
 
 
 def spans(widths):
@@ -196,8 +198,10 @@ def tile_moe_sup_lin_relu2_kernel(tc, x_words, x_scales, w1, w2_words, w2_scales
             else:
                 nc.scalar.copy(out=y[0][:, a:b], in_=first_rows[i][:])
         for i, (a, b) in enumerate(spans((BANK,) * (S // BANK))):
-            nc.scalar.copy(out=y[1][:, a:b], in_=second_layer(1, a, b, (last - i % 2) % 8)[:])
+            nc.scalar.copy(out=y[1][:, a:b], in_=second_layer(1, a, b, (last - 3 + i) % 8)[:])
 
+        identity = keep.tile([P, P], F32, name="identity")
+        make_identity(nc, identity[:])
         pieces = [(rows, a, b) for rows in range(2) for a, b in spans(TOKEN_CHUNKS[rows])]
         terms = {}
 
@@ -206,14 +210,32 @@ def tile_moe_sup_lin_relu2_kernel(tc, x_words, x_scales, w1, w2_words, w2_scales
             nc.vector.tensor_tensor(out=terms[rows, a, r][:], in0=y[rows][:].indirect(back_lists[r][:, a // 16 : b // 16]),
                                     in1=gates[:, r, a:b], op=ALU.mult)
 
-        def combine(queue, rows, a, b):
+        def combine(rows, a, b):
             res = keep.tile([P, b - a], F32, name="res%d_%d" % (rows, a))
             nc.vector.tensor_tensor(out=res[:], in0=terms[rows, a, 0][:], in1=terms[rows, a, 1][:], op=ALU.add)
-            queue.dma_start(out=out[P * rows : P * (rows + 1), a:b], in_=res[:])
+            nc.sync.dma_start(out=out[P * rows : P * (rows + 1), a:b], in_=res[:])
+
+        def combine_in_psum(i, rows, a, b):
+            blocks = spans((P,) * ((b - a) // P))
+            turned = psum.tile([P, b - a], F32, name="turned%d" % i, tag="bank%d" % (1 + 2 * (i % 2)))
+            for c, d in blocks:
+                for r in range(2):
+                    nc.tensor.matmul(turned[:, c:d], lhsT=terms[rows, a, r][:, c:d], rhs=identity[:],
+                                     start=(r == 0), stop=(r == 1), is_transpose=True)
+            summed = keep.tile([P, b - a], F32, name="summed%d" % i)
+            nc.scalar.copy(out=summed[:], in_=turned[:])
+            back = psum.tile([P, b - a], F32, name="back%d" % i, tag="bank%d" % (2 + 2 * (i % 2)))
+            for c, d in blocks:
+                nc.tensor.transpose(back[:, c:d], summed[:, c:d], identity[:])
+            res = keep.tile([P, b - a], F32, name="res%d_%d" % (rows, a))
+            nc.scalar.copy(out=res[:], in_=back[:])
+            nc.scalar.dma_start(out=out[P * rows : P * (rows + 1), a:b], in_=res[:])
 
         for i, piece in enumerate(pieces):
             fetch(0, *piece)
-            if i > 0:
-                combine(nc.sync, *pieces[i - 1])
+            if i > PSUM_PIECES:
+                combine(*pieces[i - 1])
             fetch(1, *piece)
-        combine(nc.scalar, *pieces[-1])
+            if i < PSUM_PIECES:
+                combine_in_psum(i, *piece)
+        combine(*pieces[-1])

@@ -21,12 +21,14 @@ ALU = mybir.AluOpType
 P = 128
 HALF = T // 2
 BANK = 512
-W1_CUTS = ((512,), (256, 256))
+W1_CUTS = ((2, 2), (2, 2))
+LATE = 256
 FIRST_PAIR_CUTS = (768, 768, 512)
-SECOND_PAIR_CUTS = (256,) * 8
-SLOT_CHUNKS = (256,) * 7 + (128, 128)
-PSUM_PIECES = 2
-TOKEN_CHUNKS = ((512, 512), (512, 384, 128))
+SECOND_PAIR_CUTS = (128, 384, 512, 512, 256, 128, 128)
+SLOT_CHUNKS = (256, 256, 256, 256, 512, 256, 128, 128)
+VECTOR_CHUNKS = 3
+PSUM_PIECES = 3
+TOKEN_CHUNKS = ((512, 512), (384, 384, 128, 128))
 
 
 def spans(widths):
@@ -45,83 +47,89 @@ def tile_moe_sup_lin_relu2_kernel(tc, x_words, x_scales, w1, w2_words, w2_scales
         psum = ctx.enter_context(tc.psum_pool(name="psum", bufs=1))
 
         x_plane = keep.tile([P, 2, T], U8, name="x_plane", align_bytes=64)
-        nc.vector.memset(x_plane[:].bitcast(I32), 0)
+        nc.gpsimd.memset(x_plane[:].bitcast(I32), 0)
 
-        w1_raw = [keep.tile([P, 4, H], F32, name="w1_raw%d" % s, tag="big%d" % s, align_bytes=64) for s in range(2)]
-        x_pass = [keep.tile([P, 4 * T], U8, name="x_pass%d" % s, align_bytes=64) for s in range(2)]
+        w2_plane = keep.tile([P, E, N], U8, name="w2_plane", align_bytes=64)
+        nc.gpsimd.memset(w2_plane[:].bitcast(I32), 0)
+
+        w1_raw = [keep.tile([P, 4, H], F32, name="w1_raw%d" % s, align_bytes=64) for s in range(2)]
+        x_part = {(s, h): keep.tile([P, 4 * HALF], U8, name="x_part%d%d" % (s, h), align_bytes=64) for s in range(2) for h in range(1)}
+        x_late = [keep.tile([P, 2, 4 * LATE], U8, name="x_late%d" % c, align_bytes=64) for c in range(HALF // LATE)]
         x_rows = x_words.rearrange("s p t d -> s p (t d)")
         w1_rows = w1.rearrange("(s p j) c -> s p j c", s=2, j=4)
 
         def load_w1(s):
             for a, b in spans(W1_CUTS[s]):
-                nc.sync.dma_start(out=w1_raw[s][:, :, a:b], in_=w1_rows[s, :, :, a:b])
+                nc.sync.dma_start(out=w1_raw[s][:, a:b, :], in_=w1_rows[s, :, a:b, :])
 
-        def load_x(s, a, b):
-            nc.sync.dma_start(out=x_pass[s][:, 4 * a : 4 * b].bitcast(I32), in_=x_rows[s, :, 4 * a : 4 * b].bitcast(I32))
+        def load_x(s, h):
+            nc.sync.dma_start(out=x_part[s, h][:].bitcast(I32), in_=x_rows[s, :, 4 * HALF * h : 4 * HALF * (h + 1)].bitcast(I32))
 
         load_w1(0)
         x_scale_rows = x_scales.rearrange("s (q r) t -> r q s t", r=4)
         for r in range(4):
-            nc.scalar.dma_start(out=x_plane[r:P:32, :, :].bitcast(I32), in_=x_scale_rows[r].bitcast(I32))
-        load_x(0, 0, T)
+            nc.sync.dma_start(out=x_plane[r:P:32, :, :].bitcast(I32), in_=x_scale_rows[r].bitcast(I32))
+        load_x(0, 0)
         load_w1(1)
-        load_x(1, 0, HALF)
-        load_x(1, HALF, T)
+        load_x(1, 0)
+        for c, tile in enumerate(x_late):
+            first = 4 * (HALF + LATE * c)
+            nc.sync.dma_start(out=tile[:].bitcast(I32), in_=x_rows[:, :, first : first + 4 * LATE].rearrange("s p b -> p s b").bitcast(I32))
         slot_list = lists.tile([P, S // 16], U16, name="slot_list")
         nc.sync.dma_start(slot_list[:], offs)
+        w2_scale_rows = w2_scales.rearrange("e s (q r) n -> r q (e s) n", r=4)
+        for r in range(4):
+            nc.sync.dma_start(out=w2_plane[r:P:32, :, :].bitcast(I32), in_=w2_scale_rows[r].bitcast(I32))
+        w2_codes = keep.tile([P, E, 2 * N], U8, name="w2_codes", align_bytes=64)
+        nc.sync.dma_start(out=w2_codes[:].bitcast(I32), in_=w2_words.rearrange("e s p b -> p (e s) b").bitcast(I32))
         back_lists = [lists.tile([P, T // 16], U16, name="back_list%d" % r) for r in range(2)]
         nc.sync.dma_start(back_lists[0][:], pos1)
         nc.sync.dma_start(back_lists[1][:], pos2)
+        gates = keep.tile([P, 2, T], F32, name="gates", align_bytes=64)
+        nc.sync.dma_start(out=gates[:], in_=gate.rearrange("r p t -> p r t"))
 
         w1_codes, w1_plane = {}, {}
 
         def quantise_w1(s):
-            grouped = [keep.tile([P, 2, P, 4], BF16, name="w1_grouped%d%d" % (s, u), tag="grouped%d%d" % (s, u), align_bytes=64)
+            grouped = [keep.tile([P, 2, P, 4], BF16, name="w1_grouped%d%d" % (s, u), align_bytes=64)
                        for u in range(2)]
             by_channel = w1_raw[s][:].rearrange("p j (m t) -> p m t j", t=4)
             for a, b in spans(W1_CUTS[s]):
-                ms = slice(a // 4, b // 4)
-                nc.vector.tensor_copy(out=grouped[0][:].rearrange("p t m j -> p m t j")[:, ms], in_=by_channel[:, ms, 0:2, :])
-                nc.scalar.activation(out=grouped[1][:].rearrange("p t m j -> p m t j")[:, ms], in_=by_channel[:, ms, 2:4, :], func=ACT.Copy)
+                nc.vector.tensor_copy(out=grouped[0][:].rearrange("p t m j -> p m t j")[:, :, :, a:b], in_=by_channel[:, :, 0:2, a:b])
+                nc.scalar.activation(out=grouped[1][:].rearrange("p t m j -> p m t j")[:, :, :, a:b], in_=by_channel[:, :, 2:4, a:b], func=ACT.Copy)
             for u in range(2):
                 w1_codes[s, u] = keep.tile([P, 2 * P], U32, name="w1_codes%d%d" % (s, u), align_bytes=64)
                 w1_plane[s, u] = keep.tile([P, 2 * P], U8, name="w1_plane%d%d" % (s, u), align_bytes=64)
-                for a, b in spans((1, 1) if (s, u) == (1, 0) else (2,)):
+                for a, b in spans((1, 1) if u == 0 else (2,)):
                     nc.vector.quantize_mx(
                         out=w1_codes[s, u][:, P * a : P * b].bitcast(FP8X4),
                         scales=w1_plane[s, u][:, P * a : P * b],
                         in_=grouped[u][:, a:b].rearrange("p t m j -> p (t m j)"),
                     )
 
-        sums = {(t, h): psum.tile([P, HALF], F32, name="sums%d%d" % (t, h), tag="bank%d" % (4 * (t // 2) + 2 * h + t % 2))
-                for t in range(4) for h in range(2)}
+        early_pieces = {t: spans((LATE, LATE) if t < 2 else (HALF,)) for t in range(4)}
+        early_sums = {(t, a): psum.tile([P, b - a], F32, name="early_sums%d_%d" % (t, a), tag="bank%d" % (t + 2 * (a // LATE) + 2 * (t // 2)))
+                      for t in range(4) for a, b in early_pieces[t]}
+        late_sums = {(u, c): psum.tile([P, 2, LATE], F32, name="late_sums%d%d" % (u, c), tag="bank%d" % (6 + c if u == 0 else 2 * c))
+                     for u in range(2) for c in range(HALF // LATE)}
 
-        def first_layer(s, t, h):
+        def first_layer(s, t, acc, words, a, b):
             cols = slice(P * (t % 2), P * (t % 2 + 1))
             nc.tensor.matmul_mx(
-                out=sums[t, h][:],
+                out=acc,
                 lhsT=w1_codes[s, t // 2][:, cols].bitcast(FP8X4),
                 lhsT_scale=w1_plane[s, t // 2][:, cols],
-                rhs=x_pass[s][:, 4 * HALF * h : 4 * HALF * (h + 1)].bitcast(FP8X4),
-                rhs_scale=x_plane[:, s, HALF * h : HALF * (h + 1)],
+                rhs=words.bitcast(FP8X4),
+                rhs_scale=x_plane[:, s, a:b],
                 start=(s == 0),
                 stop=(s == 1),
             )
 
         quantise_w1(0)
-        w2_plane = keep.tile([P, E, N], U8, name="w2_plane", tag="grouped00", align_bytes=64)
-        nc.vector.memset(w2_plane[:].bitcast(I32), 0)
-        w2_scale_rows = w2_scales.rearrange("e s (q r) n -> r q (e s) n", r=4)
-        for r in range(4):
-            nc.sync.dma_start(out=w2_plane[r:P:32, :, :].bitcast(I32), in_=w2_scale_rows[r].bitcast(I32))
         for t in range(4):
-            for h in range(2):
-                first_layer(0, t, h)
+            for a, b in early_pieces[t]:
+                first_layer(0, t, early_sums[t, a][:], x_part[0, 0][:, 4 * a : 4 * b], a, b)
         quantise_w1(1)
-        w2_codes = keep.tile([P, E, 2 * N], U8, name="w2_codes", tag="big0", align_bytes=64)
-        gates = keep.tile([P, 2, T], F32, name="gates", tag="big1", align_bytes=64)
-        nc.sync.dma_start(out=w2_codes[:].bitcast(I32), in_=w2_words.rearrange("e s p b -> p (e s) b").bitcast(I32))
-        nc.sync.dma_start(out=gates[:], in_=gate.rearrange("r p t -> p r t"))
 
         pairs = [keep.tile([P, T, 2], BF16, name="pairs%d" % u, align_bytes=64) for u in range(2)]
 
@@ -138,18 +146,30 @@ def tile_moe_sup_lin_relu2_kernel(tc, x_words, x_scales, w1, w2_words, w2_scales
                 nc.scalar.activation(out=dst, in_=src, func=ACT.Square)
 
         for u in range(2):
-            for t in (2 * u, 2 * u + 1):
-                for h in range(2):
-                    first_layer(1, t, h)
-            for h in range(2):
-                on_vector = (u, h) == (0, 1)
-                positive = keep.tile([P, 2, HALF], F32, name="positive%d%d" % (u, h))
-                relu(on_vector, positive[:, 0, :], sums[2 * u, h][:])
-                quarters = spans((HALF // 2, HALF // 2) if u == 0 else (HALF,))
-                for a, b in quarters:
-                    relu(on_vector, positive[:, 1, a:b], sums[2 * u + 1, h][:, a:b])
-                for a, b in quarters:
-                    square(on_vector, pairs[u][:, HALF * h + a : HALF * h + b, :], positive[:, :, a:b].rearrange("p e n -> p n e"))
+            lanes = (2 * u, 2 * u + 1)
+            for a, b in early_pieces[2 * u]:
+                for t in lanes:
+                    first_layer(1, t, early_sums[t, a][:], x_part[1, 0][:, 4 * a : 4 * b], a, b)
+            for c in range(HALF // LATE):
+                for e, t in enumerate(lanes):
+                    for s in range(2):
+                        first_layer(s, t, late_sums[u, c][:, e, :], x_late[c][:, s, :], HALF + LATE * c, HALF + LATE * (c + 1))
+            woven = keep.tile([P, HALF, 2], F32, name="woven%d" % u)
+            late = spans((LATE, LATE))
+            for a, b in early_pieces[2 * u]:
+                positive = keep.tile([P, 2, b - a], F32, name="positive%d_%d" % (u, a))
+                for e, t in enumerate(lanes):
+                    relu(a > 0, positive[:, e, :], early_sums[t, a][:])
+                if u == 1:
+                    for c, (d, f) in enumerate(late):
+                        relu(False, woven[:, d:f, :], late_sums[u, c][:].rearrange("p e n -> p n e"))
+                square(a > 0, pairs[u][:, a:b, :], positive[:].rearrange("p e n -> p n e"))
+            if u == 0:
+                for c, (d, f) in enumerate(late):
+                    relu(c == 1, woven[:, d:f, :], late_sums[u, c][:].rearrange("p e n -> p n e"))
+                    square(c == 1, pairs[u][:, HALF + d : HALF + f, :], woven[:, d:f, :])
+            else:
+                square(False, pairs[u][:, HALF:, :], woven[:])
 
         windows = [pairs[u][:].rearrange("p n e -> p (n e)").bitcast(U32) for u in range(2)]
         picked = keep.tile([P, 2, S, 2], BF16, name="picked", align_bytes=64)
@@ -193,12 +213,12 @@ def tile_moe_sup_lin_relu2_kernel(tc, x_words, x_scales, w1, w2_words, w2_scales
             first_rows.append(second_layer(0, a, b, i % 8))
         last = len(chunks) - 1
         for i, (a, b) in enumerate(chunks):
-            if i >= last - 1:
+            if i > last - VECTOR_CHUNKS:
                 nc.vector.tensor_copy(out=y[0][:, a:b], in_=first_rows[i][:])
             else:
                 nc.scalar.copy(out=y[0][:, a:b], in_=first_rows[i][:])
         for i, (a, b) in enumerate(spans((BANK,) * (S // BANK))):
-            nc.scalar.copy(out=y[1][:, a:b], in_=second_layer(1, a, b, (last - 3 + i) % 8)[:])
+            nc.scalar.copy(out=y[1][:, a:b], in_=second_layer(1, a, b, last - 3 + i)[:])
 
         identity = keep.tile([P, P], F32, name="identity")
         make_identity(nc, identity[:])

@@ -47,10 +47,10 @@ def tile_moe_sup_lin_relu2_kernel(tc, x_words, x_scales, w1, w2_words, w2_scales
         psum = ctx.enter_context(tc.psum_pool(name="psum", bufs=1))
 
         x_plane = keep.tile([P, 2, T], U8, name="x_plane", align_bytes=64)
-        nc.gpsimd.memset(x_plane[:].bitcast(I32), 0)
+        nc.vector.memset(x_plane[:].bitcast(I32), 0)
 
         w2_plane = keep.tile([P, E, N], U8, name="w2_plane", align_bytes=64)
-        nc.gpsimd.memset(w2_plane[:].bitcast(I32), 0)
+        nc.vector.memset(w2_plane[:].bitcast(I32), 0)
 
         w1_raw = [keep.tile([P, 4, H], F32, name="w1_raw%d" % s, align_bytes=64) for s in range(2)]
         x_part = {(s, h): keep.tile([P, 4 * HALF], U8, name="x_part%d%d" % (s, h), align_bytes=64) for s in range(2) for h in range(1)}
@@ -68,7 +68,7 @@ def tile_moe_sup_lin_relu2_kernel(tc, x_words, x_scales, w1, w2_words, w2_scales
         load_w1(0)
         x_scale_rows = x_scales.rearrange("s (q r) t -> r q s t", r=4)
         for r in range(4):
-            nc.sync.dma_start(out=x_plane[r:P:32, :, :].bitcast(I32), in_=x_scale_rows[r].bitcast(I32))
+            nc.scalar.dma_start(out=x_plane[r:P:32, :, :].bitcast(I32), in_=x_scale_rows[r].bitcast(I32))
         load_x(0, 0)
         load_w1(1)
         load_x(1, 0)

@@ -23,9 +23,11 @@ HALF = T // 2
 BANK = 512
 W1_CUTS = ((2, 2), (2, 2))
 LATE = 256
+SPLIT = 64
+LAST_SPLIT = 192
+AHEAD = 768
 FIRST_PAIR_CUTS = (768, 768, 512)
-SECOND_PAIR_CUTS = (128, 384, 512, 512, 256, 128, 128)
-SLOT_CHUNKS = (256, 256, 256, 256, 512, 256, 128, 128)
+SLOT_CHUNKS = (256,) * 7 + (128, 128)
 VECTOR_CHUNKS = 3
 PSUM_PIECES = 3
 TOKEN_CHUNKS = ((512, 512), (384, 384, 128, 128))
@@ -95,8 +97,16 @@ def tile_moe_sup_lin_relu2_kernel(tc, x_words, x_scales, w1, w2_words, w2_scales
                        for u in range(2)]
             by_channel = w1_raw[s][:].rearrange("p j (m t) -> p m t j", t=4)
             for a, b in spans(W1_CUTS[s]):
-                nc.vector.tensor_copy(out=grouped[0][:].rearrange("p t m j -> p m t j")[:, :, :, a:b], in_=by_channel[:, :, 0:2, a:b])
-                nc.scalar.activation(out=grouped[1][:].rearrange("p t m j -> p m t j")[:, :, :, a:b], in_=by_channel[:, :, 2:4, a:b], func=ACT.Copy)
+                for u in range(2):
+                    dst = grouped[u][:].rearrange("p t m j -> p m t j")[:, :, :, a:b]
+                    src = by_channel[:, :, 2 * u : 2 * u + 2, a:b]
+                    if (s, b, u) == (1, 4, 0):
+                        nc.vector.tensor_copy(out=dst[:, : SPLIT], in_=src[:, : SPLIT])
+                        nc.scalar.activation(out=dst[:, SPLIT :], in_=src[:, SPLIT :], func=ACT.Copy)
+                    elif u == 0:
+                        nc.vector.tensor_copy(out=dst, in_=src)
+                    else:
+                        nc.scalar.activation(out=dst, in_=src, func=ACT.Copy)
             for u in range(2):
                 w1_codes[s, u] = keep.tile([P, 2 * P], U32, name="w1_codes%d%d" % (s, u), align_bytes=64)
                 w1_plane[s, u] = keep.tile([P, 2 * P], U8, name="w1_plane%d%d" % (s, u), align_bytes=64)
@@ -113,7 +123,7 @@ def tile_moe_sup_lin_relu2_kernel(tc, x_words, x_scales, w1, w2_words, w2_scales
         late_sums = {(u, c): psum.tile([P, 2, LATE], F32, name="late_sums%d%d" % (u, c), tag="bank%d" % (6 + c if u == 0 else 2 * c))
                      for u in range(2) for c in range(HALF // LATE)}
 
-        def first_layer(s, t, acc, words, a, b):
+        def first_layer(s, t, acc, words, a, b, opens):
             cols = slice(P * (t % 2), P * (t % 2 + 1))
             nc.tensor.matmul_mx(
                 out=acc,
@@ -121,14 +131,14 @@ def tile_moe_sup_lin_relu2_kernel(tc, x_words, x_scales, w1, w2_words, w2_scales
                 lhsT_scale=w1_plane[s, t // 2][:, cols],
                 rhs=words.bitcast(FP8X4),
                 rhs_scale=x_plane[:, s, a:b],
-                start=(s == 0),
-                stop=(s == 1),
+                start=opens,
+                stop=not opens,
             )
 
         quantise_w1(0)
         for t in range(4):
             for a, b in early_pieces[t]:
-                first_layer(0, t, early_sums[t, a][:], x_part[0, 0][:, 4 * a : 4 * b], a, b)
+                first_layer(0, t, early_sums[t, a][:], x_part[0, 0][:, 4 * a : 4 * b], a, b, True)
         quantise_w1(1)
 
         pairs = [keep.tile([P, T, 2], BF16, name="pairs%d" % u, align_bytes=64) for u in range(2)]
@@ -145,35 +155,56 @@ def tile_moe_sup_lin_relu2_kernel(tc, x_words, x_scales, w1, w2_words, w2_scales
             else:
                 nc.scalar.activation(out=dst, in_=src, func=ACT.Square)
 
-        for u in range(2):
-            lanes = (2 * u, 2 * u + 1)
+        def finish_early(u):
             for a, b in early_pieces[2 * u]:
-                for t in lanes:
-                    first_layer(1, t, early_sums[t, a][:], x_part[1, 0][:, 4 * a : 4 * b], a, b)
+                for t in (2 * u, 2 * u + 1):
+                    first_layer(1, t, early_sums[t, a][:], x_part[1, 0][:, 4 * a : 4 * b], a, b, False)
+
+        def multiply_late(u):
             for c in range(HALF // LATE):
-                for e, t in enumerate(lanes):
-                    for s in range(2):
-                        first_layer(s, t, late_sums[u, c][:, e, :], x_late[c][:, s, :], HALF + LATE * c, HALF + LATE * (c + 1))
-            woven = keep.tile([P, HALF, 2], F32, name="woven%d" % u)
-            late = spans((LATE, LATE))
+                for e in range(2):
+                    for s in (1, 0):
+                        first_layer(s, 2 * u + e, late_sums[u, c][:, e, :], x_late[c][:, s, :], HALF + LATE * c, HALF + LATE * (c + 1), s == 1)
+
+        positive = [keep.tile([P, 2, HALF], F32, name="positive%d" % u, tag="relu%d" % u) for u in range(1)]
+        woven = [keep.tile([P, HALF, 2], F32, name="woven%d" % u, tag="relu%d" % (1 - u)) for u in range(1)]
+
+        def relu_early(u):
             for a, b in early_pieces[2 * u]:
-                positive = keep.tile([P, 2, b - a], F32, name="positive%d_%d" % (u, a))
-                for e, t in enumerate(lanes):
-                    relu(a > 0, positive[:, e, :], early_sums[t, a][:])
-                if u == 1:
-                    for c, (d, f) in enumerate(late):
-                        relu(False, woven[:, d:f, :], late_sums[u, c][:].rearrange("p e n -> p n e"))
-                square(a > 0, pairs[u][:, a:b, :], positive[:].rearrange("p e n -> p n e"))
-            if u == 0:
-                for c, (d, f) in enumerate(late):
-                    relu(c == 1, woven[:, d:f, :], late_sums[u, c][:].rearrange("p e n -> p n e"))
-                    square(c == 1, pairs[u][:, HALF + d : HALF + f, :], woven[:, d:f, :])
-            else:
-                square(False, pairs[u][:, HALF:, :], woven[:])
+                for e in range(2):
+                    relu(u == 0 and e == 1, positive[u][:, e, a:b], early_sums[2 * u + e, a][:])
+
+        def relu_late(u, c):
+            relu(u == 0, woven[u][:, LATE * c : LATE * (c + 1), :], late_sums[u, c][:].rearrange("p e n -> p n e"))
+
+        def square_early(u, a, b):
+            square(False, pairs[u][:, a:b, :], positive[u][:, :, a:b].rearrange("p e n -> p n e"))
+
+        def square_late(on_vector, u, a, b):
+            square(on_vector, pairs[u][:, HALF + a : HALF + b, :], woven[u][:, a:b, :])
+
+        for u in range(2):
+            finish_early(u)
+            multiply_late(u)
+        relu_early(0)
+        square_early(0, 0, LATE)
+        relu_late(0, 0)
+        square_early(0, LATE, HALF)
+        relu_late(0, 1)
+        square_late(False, 0, 0, LATE)
+        square_late(True, 0, LATE, LATE + LAST_SPLIT)
+        square_late(False, 0, LATE + LAST_SPLIT, HALF)
+        second = keep.tile([P, 2, T], F32, name="second", tag="relu1")
+        positive.append(second[:, 0, :].rearrange("p (e n) -> p e n", e=2))
+        woven.append(second[:, 1, :].rearrange("p (n e) -> p n e", e=2))
+        relu_early(1)
+        relu_late(1, 0)
+        relu_late(1, 1)
+        square_early(1, 0, HALF)
+        square_late(False, 1, 0, HALF)
 
         windows = [pairs[u][:].rearrange("p n e -> p (n e)").bitcast(U32) for u in range(2)]
-        picked = keep.tile([P, 2, S, 2], BF16, name="picked", align_bytes=64)
-        picked_words = picked[:].rearrange("p u n e -> p u (n e)").bitcast(U32)
+        picked = keep.tile([P, 4, AHEAD], U32, name="picked", align_bytes=64)
         slots = keep.tile([P, S, 4], BF16, name="slots", align_bytes=64)
         slot_words = slots[:].bitcast(U32)
         h_codes = keep.tile([P, S], U32, name="h_codes", align_bytes=64)
@@ -181,7 +212,7 @@ def tile_moe_sup_lin_relu2_kernel(tc, x_words, x_scales, w1, w2_words, w2_scales
         y = [keep.tile([P, S], F32, name="y%d" % r) for r in range(2)]
 
         def gather_pairs(u, a, b):
-            nc.vector.tensor_copy(out=picked_words[:, u, a:b], in_=windows[u].indirect(slot_list[:, a // 16 : b // 16]))
+            nc.vector.tensor_copy(out=picked[:, a // AHEAD + u, a % AHEAD : a % AHEAD + b - a], in_=windows[u].indirect(slot_list[:, a // 16 : b // 16]))
 
         def second_layer(rows, a, b, bank):
             acc = psum.tile([P, b - a], F32, name="acc%d_%d" % (rows, a), tag="bank%d" % bank)
@@ -199,26 +230,32 @@ def tile_moe_sup_lin_relu2_kernel(tc, x_words, x_scales, w1, w2_words, w2_scales
 
         for a, b in spans(FIRST_PAIR_CUTS):
             gather_pairs(0, a, b)
-        for a, b in spans(SECOND_PAIR_CUTS):
-            gather_pairs(1, a, b)
-            nc.scalar.copy(out=slot_words[:, a:b, :], in_=picked_words[:, :, a:b].rearrange("p u n -> p n u"))
-        chunks = spans(SLOT_CHUNKS)
+        chunks = [(S - b, S - a) for a, b in spans(SLOT_CHUNKS)]
         first_rows = []
-        for i, (a, b) in enumerate(chunks):
+
+        def quantise_slots(i):
+            a, b = chunks[i]
             nc.vector.quantize_mx(
                 out=h_codes[:, a:b].bitcast(FP8X4),
                 scales=h_plane[:, a:b],
                 in_=slots[:, a:b, :].rearrange("p n d -> p (n d)"),
             )
             first_rows.append(second_layer(0, a, b, i % 8))
-        last = len(chunks) - 1
-        for i, (a, b) in enumerate(chunks):
-            if i > last - VECTOR_CHUNKS:
+            if i >= len(chunks) - VECTOR_CHUNKS:
                 nc.vector.tensor_copy(out=y[0][:, a:b], in_=first_rows[i][:])
             else:
                 nc.scalar.copy(out=y[0][:, a:b], in_=first_rows[i][:])
+
+        for i, (a, b) in enumerate(chunks):
+            if i >= 3:
+                quantise_slots(i - 3)
+            gather_pairs(1, a, b)
+            both = picked[:, a // AHEAD : a // AHEAD + 2, a % AHEAD : a % AHEAD + b - a]
+            nc.scalar.copy(out=slot_words[:, a:b, :], in_=both.rearrange("p u n -> p n u"))
+        for i in range(len(chunks) - 3, len(chunks)):
+            quantise_slots(i)
         for i, (a, b) in enumerate(spans((BANK,) * (S // BANK))):
-            nc.scalar.copy(out=y[1][:, a:b], in_=second_layer(1, a, b, last - 3 + i)[:])
+            nc.scalar.copy(out=y[1][:, S - b : S - a], in_=second_layer(1, S - b, S - a, (len(chunks) - 1 - i % 2) % 8)[:])
 
         identity = keep.tile([P, P], F32, name="identity")
         make_identity(nc, identity[:])
@@ -253,9 +290,9 @@ def tile_moe_sup_lin_relu2_kernel(tc, x_words, x_scales, w1, w2_words, w2_scales
 
         for i, piece in enumerate(pieces):
             fetch(0, *piece)
+            fetch(1, *piece)
             if i > PSUM_PIECES:
                 combine(*pieces[i - 1])
-            fetch(1, *piece)
             if i < PSUM_PIECES:
                 combine_in_psum(i, *piece)
         combine(*pieces[-1])

@@ -23,14 +23,13 @@ HALF = T // 2
 BANK = 512
 W1_CUTS = ((2, 2), (2, 2))
 LATE = 256
-SPLIT = 64
 LAST_SPLIT = 192
 AHEAD = 768
 FIRST_PAIR_CUTS = (768, 768, 512)
 SLOT_CHUNKS = (256,) * 7 + (128, 128)
 VECTOR_CHUNKS = 3
-PSUM_PIECES = 3
-TOKEN_CHUNKS = ((512, 512), (384, 384, 128, 128))
+PSUM_PIECES = 2
+TOKEN_CHUNKS = ((512, 512), (512, 256, 128, 128))
 
 
 def spans(widths):
@@ -55,8 +54,7 @@ def tile_moe_sup_lin_relu2_kernel(tc, x_words, x_scales, w1, w2_words, w2_scales
         nc.vector.memset(w2_plane[:].bitcast(I32), 0)
 
         w1_raw = [keep.tile([P, 4, H], F32, name="w1_raw%d" % s, align_bytes=64) for s in range(2)]
-        x_part = {(s, h): keep.tile([P, 4 * HALF], U8, name="x_part%d%d" % (s, h), align_bytes=64) for s in range(2) for h in range(1)}
-        x_late = [keep.tile([P, 2, 4 * LATE], U8, name="x_late%d" % c, align_bytes=64) for c in range(HALF // LATE)]
+        x_part = {(s, h): keep.tile([P, 4 * HALF], U8, name="x_part%d%d" % (s, h), align_bytes=64) for s in range(2) for h in range(2)}
         x_rows = x_words.rearrange("s p t d -> s p (t d)")
         w1_rows = w1.rearrange("(s p j) c -> s p j c", s=2, j=4)
 
@@ -74,9 +72,8 @@ def tile_moe_sup_lin_relu2_kernel(tc, x_words, x_scales, w1, w2_words, w2_scales
         load_x(0, 0)
         load_w1(1)
         load_x(1, 0)
-        for c, tile in enumerate(x_late):
-            first = 4 * (HALF + LATE * c)
-            nc.sync.dma_start(out=tile[:].bitcast(I32), in_=x_rows[:, :, first : first + 4 * LATE].rearrange("s p b -> p s b").bitcast(I32))
+        load_x(1, 1)
+        load_x(0, 1)
         slot_list = lists.tile([P, S // 16], U16, name="slot_list")
         nc.sync.dma_start(slot_list[:], offs)
         w2_scale_rows = w2_scales.rearrange("e s (q r) n -> r q (e s) n", r=4)
@@ -97,16 +94,8 @@ def tile_moe_sup_lin_relu2_kernel(tc, x_words, x_scales, w1, w2_words, w2_scales
                        for u in range(2)]
             by_channel = w1_raw[s][:].rearrange("p j (m t) -> p m t j", t=4)
             for a, b in spans(W1_CUTS[s]):
-                for u in range(2):
-                    dst = grouped[u][:].rearrange("p t m j -> p m t j")[:, :, :, a:b]
-                    src = by_channel[:, :, 2 * u : 2 * u + 2, a:b]
-                    if (s, b, u) == (1, 4, 0):
-                        nc.vector.tensor_copy(out=dst[:, : SPLIT], in_=src[:, : SPLIT])
-                        nc.scalar.activation(out=dst[:, SPLIT :], in_=src[:, SPLIT :], func=ACT.Copy)
-                    elif u == 0:
-                        nc.vector.tensor_copy(out=dst, in_=src)
-                    else:
-                        nc.scalar.activation(out=dst, in_=src, func=ACT.Copy)
+                nc.vector.tensor_copy(out=grouped[0][:].rearrange("p t m j -> p m t j")[:, :, :, a:b], in_=by_channel[:, :, 0:2, a:b])
+                nc.scalar.activation(out=grouped[1][:].rearrange("p t m j -> p m t j")[:, :, :, a:b], in_=by_channel[:, :, 2:4, a:b], func=ACT.Copy)
             for u in range(2):
                 w1_codes[s, u] = keep.tile([P, 2 * P], U32, name="w1_codes%d%d" % (s, u), align_bytes=64)
                 w1_plane[s, u] = keep.tile([P, 2 * P], U8, name="w1_plane%d%d" % (s, u), align_bytes=64)
@@ -164,7 +153,7 @@ def tile_moe_sup_lin_relu2_kernel(tc, x_words, x_scales, w1, w2_words, w2_scales
             for c in range(HALF // LATE):
                 for e in range(2):
                     for s in (1, 0):
-                        first_layer(s, 2 * u + e, late_sums[u, c][:, e, :], x_late[c][:, s, :], HALF + LATE * c, HALF + LATE * (c + 1), s == 1)
+                        first_layer(s, 2 * u + e, late_sums[u, c][:, e, :], x_part[s, 1][:, 4 * LATE * c : 4 * LATE * (c + 1)], HALF + LATE * c, HALF + LATE * (c + 1), s == 1)
 
         positive = [keep.tile([P, 2, HALF], F32, name="positive%d" % u, tag="relu%d" % u) for u in range(1)]
         woven = [keep.tile([P, HALF, 2], F32, name="woven%d" % u, tag="relu%d" % (1 - u)) for u in range(1)]
@@ -274,7 +263,7 @@ def tile_moe_sup_lin_relu2_kernel(tc, x_words, x_scales, w1, w2_words, w2_scales
 
         def combine_in_psum(i, rows, a, b):
             blocks = spans((P,) * ((b - a) // P))
-            turned = psum.tile([P, b - a], F32, name="turned%d" % i, tag="bank%d" % (1 + 2 * (i % 2)))
+            turned = psum.tile([P, b - a], F32, name="turned%d" % i, tag="bank%d" % (7 * i))
             for c, d in blocks:
                 for r in range(2):
                     nc.tensor.matmul(turned[:, c:d], lhsT=terms[rows, a, r][:, c:d], rhs=identity[:],

@@ -20,16 +20,16 @@ ALU = mybir.AluOpType
 
 P = 128
 HALF = T // 2
-BANK = 512
 W1_CUTS = ((2, 2), (2, 2))
 LATE = 256
-LAST_SPLIT = 192
-AHEAD = 768
-FIRST_PAIR_CUTS = (768, 768, 512)
+LAST_SPLIT = 160
+AHEAD = 1024
+LAG = 4
+FIRST_PAIR_CUTS = (512,) * 4
 SLOT_CHUNKS = (256,) * 7 + (128, 128)
-VECTOR_CHUNKS = 3
-PSUM_PIECES = 2
-TOKEN_CHUNKS = ((512, 512), (512, 256, 128, 128))
+VECTOR_CHUNKS = 4
+PSUM_PIECES = 5
+TOKEN_CHUNKS = ((384, 384, 256), (256, 128, 384, 192, 64))
 
 
 def spans(widths):
@@ -193,18 +193,17 @@ def tile_moe_sup_lin_relu2_kernel(tc, x_words, x_scales, w1, w2_words, w2_scales
         square_late(False, 1, 0, HALF)
 
         windows = [pairs[u][:].rearrange("p n e -> p (n e)").bitcast(U32) for u in range(2)]
-        picked = keep.tile([P, 4, AHEAD], U32, name="picked", align_bytes=64)
+        picked = keep.tile([P, 3, AHEAD], U32, name="picked", tag="picked", align_bytes=64)
         slots = keep.tile([P, S, 4], BF16, name="slots", align_bytes=64)
         slot_words = slots[:].bitcast(U32)
         h_codes = keep.tile([P, S], U32, name="h_codes", align_bytes=64)
         h_plane = keep.tile([P, S], U8, name="h_plane", align_bytes=64)
-        y = [keep.tile([P, S], F32, name="y%d" % r) for r in range(2)]
+        y = [keep.tile([P, S], F32, name="y0")]
 
         def gather_pairs(u, a, b):
             nc.vector.tensor_copy(out=picked[:, a // AHEAD + u, a % AHEAD : a % AHEAD + b - a], in_=windows[u].indirect(slot_list[:, a // 16 : b // 16]))
 
-        def second_layer(rows, a, b, bank):
-            acc = psum.tile([P, b - a], F32, name="acc%d_%d" % (rows, a), tag="bank%d" % bank)
+        def second_layer(rows, a, b, acc):
             for e in range(a // C, b // C):
                 nc.tensor.matmul_mx(
                     out=acc[:, C * e - a : C * (e + 1) - a],
@@ -215,12 +214,11 @@ def tile_moe_sup_lin_relu2_kernel(tc, x_words, x_scales, w1, w2_words, w2_scales
                     start=True,
                     stop=True,
                 )
-            return acc
 
         for a, b in spans(FIRST_PAIR_CUTS):
             gather_pairs(0, a, b)
         chunks = [(S - b, S - a) for a, b in spans(SLOT_CHUNKS)]
-        first_rows = []
+        held = {}
 
         def quantise_slots(i):
             a, b = chunks[i]
@@ -229,22 +227,32 @@ def tile_moe_sup_lin_relu2_kernel(tc, x_words, x_scales, w1, w2_words, w2_scales
                 scales=h_plane[:, a:b],
                 in_=slots[:, a:b, :].rearrange("p n d -> p (n d)"),
             )
-            first_rows.append(second_layer(0, a, b, i % 8))
+            acc = psum.tile([P, 2, b - a], F32, name="acc%d" % i, tag="bank%d" % (i % 8))
+            second_layer(0, a, b, acc[:, 0, :])
+            if 0 < i < len(chunks) - LAG:
+                second_layer(1, a, b, acc[:, 1, :])
+                held[i] = acc
             if i >= len(chunks) - VECTOR_CHUNKS:
-                nc.vector.tensor_copy(out=y[0][:, a:b], in_=first_rows[i][:])
+                nc.vector.tensor_copy(out=y[0][:, a:b], in_=acc[:, 0, :])
             else:
-                nc.scalar.copy(out=y[0][:, a:b], in_=first_rows[i][:])
+                nc.scalar.copy(out=y[0][:, a:b], in_=acc[:, 0, :])
 
         for i, (a, b) in enumerate(chunks):
-            if i >= 3:
-                quantise_slots(i - 3)
+            if i >= LAG:
+                quantise_slots(i - LAG)
             gather_pairs(1, a, b)
             both = picked[:, a // AHEAD : a // AHEAD + 2, a % AHEAD : a % AHEAD + b - a]
             nc.scalar.copy(out=slot_words[:, a:b, :], in_=both.rearrange("p u n -> p n u"))
-        for i in range(len(chunks) - 3, len(chunks)):
+        for i in range(len(chunks) - LAG, len(chunks)):
             quantise_slots(i)
-        for i, (a, b) in enumerate(spans((BANK,) * (S // BANK))):
-            nc.scalar.copy(out=y[1][:, S - b : S - a], in_=second_layer(1, S - b, S - a, (len(chunks) - 1 - i % 2) % 8)[:])
+        y.append(keep.tile([P, S], F32, name="y1", tag="picked", align_bytes=64))
+        for i, acc in held.items():
+            a, b = chunks[i]
+            nc.scalar.copy(out=y[1][:, a:b], in_=acc[:, 1, :])
+        for bank, (a, b) in ((5, chunks[5]), (6, chunks[6]), (7, (0, 2 * C)), (0, chunks[0])):
+            acc = psum.tile([P, b - a], F32, name="late_acc%d" % bank, tag="bank%d" % bank)
+            second_layer(1, a, b, acc)
+            nc.scalar.copy(out=y[1][:, a:b], in_=acc[:])
 
         identity = keep.tile([P, P], F32, name="identity")
         make_identity(nc, identity[:])
@@ -263,14 +271,14 @@ def tile_moe_sup_lin_relu2_kernel(tc, x_words, x_scales, w1, w2_words, w2_scales
 
         def combine_in_psum(i, rows, a, b):
             blocks = spans((P,) * ((b - a) // P))
-            turned = psum.tile([P, b - a], F32, name="turned%d" % i, tag="bank%d" % (7 * i))
+            turned = psum.tile([P, b - a], F32, name="turned%d" % i, tag="bank%d" % (i % 2))
             for c, d in blocks:
                 for r in range(2):
                     nc.tensor.matmul(turned[:, c:d], lhsT=terms[rows, a, r][:, c:d], rhs=identity[:],
                                      start=(r == 0), stop=(r == 1), is_transpose=True)
             summed = keep.tile([P, b - a], F32, name="summed%d" % i)
             nc.scalar.copy(out=summed[:], in_=turned[:])
-            back = psum.tile([P, b - a], F32, name="back%d" % i, tag="bank%d" % (2 + 2 * (i % 2)))
+            back = psum.tile([P, b - a], F32, name="back%d" % i, tag="bank%d" % (2 + i % 2))
             for c, d in blocks:
                 nc.tensor.transpose(back[:, c:d], summed[:, c:d], identity[:])
             res = keep.tile([P, b - a], F32, name="res%d_%d" % (rows, a))

@@ -19,17 +19,16 @@ ACT = mybir.ActivationFunctionType
 ALU = mybir.AluOpType
 
 P = 128
+BANKS = 8
 HALF = T // 2
-W1_CUTS = ((2, 2), (2, 2))
-LATE = 256
-LAST_SPLIT = 160
-AHEAD = 1024
-LAG = 4
-FIRST_PAIR_CUTS = (512,) * 4
+QUARTER = T // 4
+VECTOR_SQUARES = 160
+FIRST_PAIR_CUTS = (768, 768, 512)
 SLOT_CHUNKS = (256,) * 7 + (128, 128)
-VECTOR_CHUNKS = 4
-PSUM_PIECES = 5
-TOKEN_CHUNKS = ((384, 384, 256), (256, 128, 384, 192, 64))
+LAG = 4
+AHEAD = 1024
+TOKEN_PIECES = ((384, 384, 256), (384, 448, 128, 64))
+PSUM_PIECES = 4
 
 
 def spans(widths):
@@ -49,7 +48,6 @@ def tile_moe_sup_lin_relu2_kernel(tc, x_words, x_scales, w1, w2_words, w2_scales
 
         x_plane = keep.tile([P, 2, T], U8, name="x_plane", align_bytes=64)
         nc.vector.memset(x_plane[:].bitcast(I32), 0)
-
         w2_plane = keep.tile([P, E, N], U8, name="w2_plane", align_bytes=64)
         nc.vector.memset(w2_plane[:].bitcast(I32), 0)
 
@@ -57,9 +55,10 @@ def tile_moe_sup_lin_relu2_kernel(tc, x_words, x_scales, w1, w2_words, w2_scales
         x_part = {(s, h): keep.tile([P, 4 * HALF], U8, name="x_part%d%d" % (s, h), align_bytes=64) for s in range(2) for h in range(2)}
         x_rows = x_words.rearrange("s p t d -> s p (t d)")
         w1_rows = w1.rearrange("(s p j) c -> s p j c", s=2, j=4)
+        row_pairs = spans((2, 2))
 
         def load_w1(s):
-            for a, b in spans(W1_CUTS[s]):
+            for a, b in row_pairs:
                 nc.sync.dma_start(out=w1_raw[s][:, a:b, :], in_=w1_rows[s, :, a:b, :])
 
         def load_x(s, h):
@@ -90,12 +89,11 @@ def tile_moe_sup_lin_relu2_kernel(tc, x_words, x_scales, w1, w2_words, w2_scales
         w1_codes, w1_plane = {}, {}
 
         def quantise_w1(s):
-            grouped = [keep.tile([P, 2, P, 4], BF16, name="w1_grouped%d%d" % (s, u), align_bytes=64)
-                       for u in range(2)]
-            by_channel = w1_raw[s][:].rearrange("p j (m t) -> p m t j", t=4)
-            for a, b in spans(W1_CUTS[s]):
-                nc.vector.tensor_copy(out=grouped[0][:].rearrange("p t m j -> p m t j")[:, :, :, a:b], in_=by_channel[:, :, 0:2, a:b])
-                nc.scalar.activation(out=grouped[1][:].rearrange("p t m j -> p m t j")[:, :, :, a:b], in_=by_channel[:, :, 2:4, a:b], func=ACT.Copy)
+            grouped = [keep.tile([P, 2, P, 4], BF16, name="w1_grouped%d%d" % (s, u), align_bytes=64) for u in range(2)]
+            by_lane = w1_raw[s][:].rearrange("p j (m t) -> p m t j", t=4)
+            for a, b in row_pairs:
+                nc.vector.tensor_copy(out=grouped[0][:].rearrange("p e m j -> p m e j")[:, :, :, a:b], in_=by_lane[:, :, 0:2, a:b])
+                nc.scalar.activation(out=grouped[1][:].rearrange("p e m j -> p m e j")[:, :, :, a:b], in_=by_lane[:, :, 2:4, a:b], func=ACT.Copy)
             for u in range(2):
                 w1_codes[s, u] = keep.tile([P, 2 * P], U32, name="w1_codes%d%d" % (s, u), align_bytes=64)
                 w1_plane[s, u] = keep.tile([P, 2 * P], U8, name="w1_plane%d%d" % (s, u), align_bytes=64)
@@ -103,22 +101,23 @@ def tile_moe_sup_lin_relu2_kernel(tc, x_words, x_scales, w1, w2_words, w2_scales
                     nc.vector.quantize_mx(
                         out=w1_codes[s, u][:, P * a : P * b].bitcast(FP8X4),
                         scales=w1_plane[s, u][:, P * a : P * b],
-                        in_=grouped[u][:, a:b].rearrange("p t m j -> p (t m j)"),
+                        in_=grouped[u][:, a:b].rearrange("p e m j -> p (e m j)"),
                     )
 
-        early_pieces = {t: spans((LATE, LATE) if t < 2 else (HALF,)) for t in range(4)}
-        early_sums = {(t, a): psum.tile([P, b - a], F32, name="early_sums%d_%d" % (t, a), tag="bank%d" % (t + 2 * (a // LATE) + 2 * (t // 2)))
+        early_pieces = {t: spans((QUARTER, QUARTER) if t < 2 else (HALF,)) for t in range(4)}
+        early_sums = {(t, a): psum.tile([P, b - a], F32, name="early_sums%d_%d" % (t, a), tag="bank%d" % (t + 2 * (a // QUARTER) + 2 * (t // 2)))
                       for t in range(4) for a, b in early_pieces[t]}
-        late_sums = {(u, c): psum.tile([P, 2, LATE], F32, name="late_sums%d%d" % (u, c), tag="bank%d" % (6 + c if u == 0 else 2 * c))
-                     for u in range(2) for c in range(HALF // LATE)}
+        late_sums = {(u, c): psum.tile([P, 2, QUARTER], F32, name="late_sums%d%d" % (u, c), tag="bank%d" % (6 + c if u == 0 else 2 * c))
+                     for u in range(2) for c in range(2)}
 
-        def first_layer(s, t, acc, words, a, b, opens):
+        def first_layer(s, t, acc, a, b, opens):
             cols = slice(P * (t % 2), P * (t % 2 + 1))
+            first = a % HALF
             nc.tensor.matmul_mx(
                 out=acc,
                 lhsT=w1_codes[s, t // 2][:, cols].bitcast(FP8X4),
                 lhsT_scale=w1_plane[s, t // 2][:, cols],
-                rhs=words.bitcast(FP8X4),
+                rhs=x_part[s, a // HALF][:, 4 * first : 4 * (first + b - a)].bitcast(FP8X4),
                 rhs_scale=x_plane[:, s, a:b],
                 start=opens,
                 stop=not opens,
@@ -127,8 +126,16 @@ def tile_moe_sup_lin_relu2_kernel(tc, x_words, x_scales, w1, w2_words, w2_scales
         quantise_w1(0)
         for t in range(4):
             for a, b in early_pieces[t]:
-                first_layer(0, t, early_sums[t, a][:], x_part[0, 0][:, 4 * a : 4 * b], a, b, True)
+                first_layer(0, t, early_sums[t, a][:], a, b, True)
         quantise_w1(1)
+        for u in range(2):
+            for a, b in early_pieces[2 * u]:
+                for t in (2 * u, 2 * u + 1):
+                    first_layer(1, t, early_sums[t, a][:], a, b, False)
+            for c in range(2):
+                for e in range(2):
+                    for s in (1, 0):
+                        first_layer(s, 2 * u + e, late_sums[u, c][:, e, :], HALF + QUARTER * c, HALF + QUARTER * (c + 1), s == 1)
 
         pairs = [keep.tile([P, T, 2], BF16, name="pairs%d" % u, align_bytes=64) for u in range(2)]
 
@@ -144,47 +151,33 @@ def tile_moe_sup_lin_relu2_kernel(tc, x_words, x_scales, w1, w2_words, w2_scales
             else:
                 nc.scalar.activation(out=dst, in_=src, func=ACT.Square)
 
-        def finish_early(u):
-            for a, b in early_pieces[2 * u]:
-                for t in (2 * u, 2 * u + 1):
-                    first_layer(1, t, early_sums[t, a][:], x_part[1, 0][:, 4 * a : 4 * b], a, b, False)
-
-        def multiply_late(u):
-            for c in range(HALF // LATE):
-                for e in range(2):
-                    for s in (1, 0):
-                        first_layer(s, 2 * u + e, late_sums[u, c][:, e, :], x_part[s, 1][:, 4 * LATE * c : 4 * LATE * (c + 1)], HALF + LATE * c, HALF + LATE * (c + 1), s == 1)
-
-        positive = [keep.tile([P, 2, HALF], F32, name="positive%d" % u, tag="relu%d" % u) for u in range(1)]
-        woven = [keep.tile([P, HALF, 2], F32, name="woven%d" % u, tag="relu%d" % (1 - u)) for u in range(1)]
+        apart = [keep.tile([P, 2, HALF], F32, name="apart0")]
+        woven = [keep.tile([P, HALF, 2], F32, name="woven0", tag="relu")]
 
         def relu_early(u):
             for a, b in early_pieces[2 * u]:
                 for e in range(2):
-                    relu(u == 0 and e == 1, positive[u][:, e, a:b], early_sums[2 * u + e, a][:])
+                    relu(u == 0 and e == 1, apart[u][:, e, a:b], early_sums[2 * u + e, a][:])
 
         def relu_late(u, c):
-            relu(u == 0, woven[u][:, LATE * c : LATE * (c + 1), :], late_sums[u, c][:].rearrange("p e n -> p n e"))
+            relu(u == 0, woven[u][:, QUARTER * c : QUARTER * (c + 1), :], late_sums[u, c][:].rearrange("p e n -> p n e"))
 
         def square_early(u, a, b):
-            square(False, pairs[u][:, a:b, :], positive[u][:, :, a:b].rearrange("p e n -> p n e"))
+            square(False, pairs[u][:, a:b, :], apart[u][:, :, a:b].rearrange("p e n -> p n e"))
 
         def square_late(on_vector, u, a, b):
             square(on_vector, pairs[u][:, HALF + a : HALF + b, :], woven[u][:, a:b, :])
 
-        for u in range(2):
-            finish_early(u)
-            multiply_late(u)
         relu_early(0)
-        square_early(0, 0, LATE)
+        square_early(0, 0, QUARTER)
         relu_late(0, 0)
-        square_early(0, LATE, HALF)
+        square_early(0, QUARTER, HALF)
         relu_late(0, 1)
-        square_late(False, 0, 0, LATE)
-        square_late(True, 0, LATE, LATE + LAST_SPLIT)
-        square_late(False, 0, LATE + LAST_SPLIT, HALF)
-        second = keep.tile([P, 2, T], F32, name="second", tag="relu1")
-        positive.append(second[:, 0, :].rearrange("p (e n) -> p e n", e=2))
+        square_late(False, 0, 0, QUARTER)
+        square_late(True, 0, QUARTER, QUARTER + VECTOR_SQUARES)
+        square_late(False, 0, QUARTER + VECTOR_SQUARES, HALF)
+        second = keep.tile([P, 2, T], F32, name="second", tag="relu")
+        apart.append(second[:, 0, :].rearrange("p (e n) -> p e n", e=2))
         woven.append(second[:, 1, :].rearrange("p (n e) -> p n e", e=2))
         relu_early(1)
         relu_late(1, 0)
@@ -193,7 +186,8 @@ def tile_moe_sup_lin_relu2_kernel(tc, x_words, x_scales, w1, w2_words, w2_scales
         square_late(False, 1, 0, HALF)
 
         windows = [pairs[u][:].rearrange("p n e -> p (n e)").bitcast(U32) for u in range(2)]
-        picked = keep.tile([P, 3, AHEAD], U32, name="picked", tag="picked", align_bytes=64)
+        picked = keep.tile([P, S // AHEAD + 1, AHEAD], U32, name="picked", tag="picked", align_bytes=64)
+        picked_run = picked[:].rearrange("p r n -> p (r n)")
         slots = keep.tile([P, S, 4], BF16, name="slots", align_bytes=64)
         slot_words = slots[:].bitcast(U32)
         h_codes = keep.tile([P, S], U32, name="h_codes", align_bytes=64)
@@ -201,7 +195,7 @@ def tile_moe_sup_lin_relu2_kernel(tc, x_words, x_scales, w1, w2_words, w2_scales
         y = [keep.tile([P, S], F32, name="y0")]
 
         def gather_pairs(u, a, b):
-            nc.vector.tensor_copy(out=picked[:, a // AHEAD + u, a % AHEAD : a % AHEAD + b - a], in_=windows[u].indirect(slot_list[:, a // 16 : b // 16]))
+            nc.vector.tensor_copy(out=picked_run[:, AHEAD * u + a : AHEAD * u + b], in_=windows[u].indirect(slot_list[:, a // 16 : b // 16]))
 
         def second_layer(rows, a, b, acc):
             for e in range(a // C, b // C):
@@ -218,6 +212,7 @@ def tile_moe_sup_lin_relu2_kernel(tc, x_words, x_scales, w1, w2_words, w2_scales
         for a, b in spans(FIRST_PAIR_CUTS):
             gather_pairs(0, a, b)
         chunks = [(S - b, S - a) for a, b in spans(SLOT_CHUNKS)]
+        tail = len(chunks) - LAG
         held = {}
 
         def quantise_slots(i):
@@ -225,14 +220,14 @@ def tile_moe_sup_lin_relu2_kernel(tc, x_words, x_scales, w1, w2_words, w2_scales
             nc.vector.quantize_mx(
                 out=h_codes[:, a:b].bitcast(FP8X4),
                 scales=h_plane[:, a:b],
-                in_=slots[:, a:b, :].rearrange("p n d -> p (n d)"),
+                in_=slots[:, a:b, :].rearrange("p n t -> p (n t)"),
             )
-            acc = psum.tile([P, 2, b - a], F32, name="acc%d" % i, tag="bank%d" % (i % 8))
+            acc = psum.tile([P, 2, b - a], F32, name="acc%d" % i, tag="bank%d" % (i % BANKS))
             second_layer(0, a, b, acc[:, 0, :])
-            if 0 < i < len(chunks) - LAG:
+            if 0 < i < tail:
                 second_layer(1, a, b, acc[:, 1, :])
                 held[i] = acc
-            if i >= len(chunks) - VECTOR_CHUNKS:
+            if i >= tail:
                 nc.vector.tensor_copy(out=y[0][:, a:b], in_=acc[:, 0, :])
             else:
                 nc.scalar.copy(out=y[0][:, a:b], in_=acc[:, 0, :])
@@ -243,20 +238,22 @@ def tile_moe_sup_lin_relu2_kernel(tc, x_words, x_scales, w1, w2_words, w2_scales
             gather_pairs(1, a, b)
             both = picked[:, a // AHEAD : a // AHEAD + 2, a % AHEAD : a % AHEAD + b - a]
             nc.scalar.copy(out=slot_words[:, a:b, :], in_=both.rearrange("p u n -> p n u"))
-        for i in range(len(chunks) - LAG, len(chunks)):
+        for i in range(tail, len(chunks)):
             quantise_slots(i)
+
         y.append(keep.tile([P, S], F32, name="y1", tag="picked", align_bytes=64))
         for i, acc in held.items():
             a, b = chunks[i]
             nc.scalar.copy(out=y[1][:, a:b], in_=acc[:, 1, :])
-        for bank, (a, b) in ((5, chunks[5]), (6, chunks[6]), (7, (0, 2 * C)), (0, chunks[0])):
-            acc = psum.tile([P, b - a], F32, name="late_acc%d" % bank, tag="bank%d" % bank)
+        left = [(tail, chunks[tail]), (tail + 1, chunks[tail + 1]), (tail + 2, (0, 2 * C)), (tail + 3, chunks[0])]
+        for i, (a, b) in left:
+            acc = psum.tile([P, b - a], F32, name="left_acc%d" % i, tag="bank%d" % (i % BANKS))
             second_layer(1, a, b, acc)
             nc.scalar.copy(out=y[1][:, a:b], in_=acc[:])
 
         identity = keep.tile([P, P], F32, name="identity")
         make_identity(nc, identity[:])
-        pieces = [(rows, a, b) for rows in range(2) for a, b in spans(TOKEN_CHUNKS[rows])]
+        pieces = [(rows, a, b) for rows in range(2) for a, b in spans(TOKEN_PIECES[rows])]
         terms = {}
 
         def fetch(r, rows, a, b):
@@ -288,8 +285,8 @@ def tile_moe_sup_lin_relu2_kernel(tc, x_words, x_scales, w1, w2_words, w2_scales
         for i, piece in enumerate(pieces):
             fetch(0, *piece)
             fetch(1, *piece)
-            if i > PSUM_PIECES:
-                combine(*pieces[i - 1])
             if i < PSUM_PIECES:
                 combine_in_psum(i, *piece)
+            elif i > PSUM_PIECES:
+                combine(*pieces[i - 1])
         combine(*pieces[-1])

@@ -22,7 +22,7 @@ P = 128
 BANKS = 8
 HALF = T // 2
 QUARTER = T // 4
-VECTOR_SQUARES = 160
+VECTOR_SQUARES = (112, 112, 112, 96)
 FIRST_PAIR_CUTS = (768, 768, 512)
 SLOT_CHUNKS = (256,) * 7 + (128, 128)
 LAG = 4
@@ -46,13 +46,14 @@ def tile_moe_sup_lin_relu2_kernel(tc, x_words, x_scales, w1, w2_words, w2_scales
         keep = ctx.enter_context(tc.tile_pool(name="keep", bufs=1))
         psum = ctx.enter_context(tc.psum_pool(name="psum", bufs=1))
 
-        x_plane = keep.tile([P, 2, T], U8, name="x_plane", align_bytes=64)
+        x_plane = keep.tile([P, T], U8, name="x_plane", align_bytes=64)
         nc.vector.memset(x_plane[:].bitcast(I32), 0)
         w2_plane = keep.tile([P, E, N], U8, name="w2_plane", align_bytes=64)
         nc.vector.memset(w2_plane[:].bitcast(I32), 0)
 
         w1_raw = [keep.tile([P, 4, H], F32, name="w1_raw%d" % s, align_bytes=64) for s in range(2)]
-        x_part = {(s, h): keep.tile([P, 4 * HALF], U8, name="x_part%d%d" % (s, h), align_bytes=64) for s in range(2) for h in range(2)}
+        x_early = [keep.tile([P, 4 * HALF], U8, name="x_early%d" % s, align_bytes=64) for s in range(2)]
+        x_late = [keep.tile([P, 2, 4 * QUARTER], U8, name="x_late%d" % c, align_bytes=64) for c in range(2)]
         x_rows = x_words.rearrange("s p t d -> s p (t d)")
         w1_rows = w1.rearrange("(s p j) c -> s p j c", s=2, j=4)
         row_pairs = spans((2, 2))
@@ -61,18 +62,21 @@ def tile_moe_sup_lin_relu2_kernel(tc, x_words, x_scales, w1, w2_words, w2_scales
             for a, b in row_pairs:
                 nc.sync.dma_start(out=w1_raw[s][:, a:b, :], in_=w1_rows[s, :, a:b, :])
 
-        def load_x(s, h):
-            nc.sync.dma_start(out=x_part[s, h][:].bitcast(I32), in_=x_rows[s, :, 4 * HALF * h : 4 * HALF * (h + 1)].bitcast(I32))
+        def load_early(s):
+            nc.sync.dma_start(out=x_early[s][:].bitcast(I32), in_=x_rows[s, :, 0 : 4 * HALF].bitcast(I32))
+
+        def load_late(c):
+            a = 4 * (HALF + QUARTER * c)
+            nc.sync.dma_start(out=x_late[c][:].bitcast(I32), in_=x_rows[:, :, a : a + 4 * QUARTER].rearrange("s p b -> p s b").bitcast(I32))
 
         load_w1(0)
-        x_scale_rows = x_scales.rearrange("s (q r) t -> r q s t", r=4)
-        for r in range(4):
-            nc.scalar.dma_start(out=x_plane[r:P:32, :, :].bitcast(I32), in_=x_scale_rows[r].bitcast(I32))
-        load_x(0, 0)
+        for q in range(4):
+            nc.scalar.dma_start(out=x_plane[32 * q : 32 * q + 8, :].bitcast(I32), in_=x_scales[:, 4 * q : 4 * q + 4, :].bitcast(I32))
+        load_early(0)
         load_w1(1)
-        load_x(1, 0)
-        load_x(1, 1)
-        load_x(0, 1)
+        load_early(1)
+        load_late(0)
+        load_late(1)
         slot_list = lists.tile([P, S // 16], U16, name="slot_list")
         nc.sync.dma_start(slot_list[:], offs)
         w2_scale_rows = w2_scales.rearrange("e s (q r) n -> r q (e s) n", r=4)
@@ -104,38 +108,39 @@ def tile_moe_sup_lin_relu2_kernel(tc, x_words, x_scales, w1, w2_words, w2_scales
                         in_=grouped[u][:, a:b].rearrange("p e m j -> p (e m j)"),
                     )
 
-        early_pieces = {t: spans((QUARTER, QUARTER) if t < 2 else (HALF,)) for t in range(4)}
-        early_sums = {(t, a): psum.tile([P, b - a], F32, name="early_sums%d_%d" % (t, a), tag="bank%d" % (t + 2 * (a // QUARTER) + 2 * (t // 2)))
-                      for t in range(4) for a, b in early_pieces[t]}
-        late_sums = {(u, c): psum.tile([P, 2, QUARTER], F32, name="late_sums%d%d" % (u, c), tag="bank%d" % (6 + c if u == 0 else 2 * c))
-                     for u in range(2) for c in range(2)}
+        sums = {(t, q): psum.tile([P, QUARTER], F32, name="sums%d_%d" % (t, q), tag="bank%d" % ((0, 2, 6, 0)[q] + t))
+                for q in range(4) for t in range(2)}
+        early_sums = {t: psum.tile([P, HALF], F32, name="early_sums%d" % t, tag="bank%d" % (t + 2)) for t in (2, 3)}
+        late_sums = [psum.tile([P, 2, QUARTER], F32, name="late_sums%d" % c, tag="bank%d" % (2 + c)) for c in range(2)]
+        quarters = spans((QUARTER,) * 4)
 
         def first_layer(s, t, acc, a, b, opens):
             cols = slice(P * (t % 2), P * (t % 2 + 1))
-            first = a % HALF
+            words = x_early[s][:, 4 * a : 4 * b] if a < HALF else x_late[(a - HALF) // QUARTER][:, s, :]
             nc.tensor.matmul_mx(
                 out=acc,
                 lhsT=w1_codes[s, t // 2][:, cols].bitcast(FP8X4),
                 lhsT_scale=w1_plane[s, t // 2][:, cols],
-                rhs=x_part[s, a // HALF][:, 4 * first : 4 * (first + b - a)].bitcast(FP8X4),
-                rhs_scale=x_plane[:, s, a:b],
+                rhs=words.bitcast(FP8X4),
+                rhs_scale=x_plane[4 * s : P, a:b],
                 start=opens,
                 stop=not opens,
             )
 
         quantise_w1(0)
-        for t in range(4):
-            for a, b in early_pieces[t]:
-                first_layer(0, t, early_sums[t, a][:], a, b, True)
+        for t in range(2):
+            for q in range(2):
+                first_layer(0, t, sums[t, q][:], *quarters[q], True)
+        for t in (2, 3):
+            first_layer(0, t, early_sums[t][:], 0, HALF, True)
         quantise_w1(1)
-        for u in range(2):
-            for a, b in early_pieces[2 * u]:
-                for t in (2 * u, 2 * u + 1):
-                    first_layer(1, t, early_sums[t, a][:], a, b, False)
-            for c in range(2):
-                for e in range(2):
-                    for s in (1, 0):
-                        first_layer(s, 2 * u + e, late_sums[u, c][:, e, :], HALF + QUARTER * c, HALF + QUARTER * (c + 1), s == 1)
+        for q in range(2):
+            for t in range(2):
+                first_layer(1, t, sums[t, q][:], *quarters[q], False)
+
+        def late_group(t, acc, q):
+            for s in (1, 0):
+                first_layer(s, t, acc, *quarters[q], s == 1)
 
         pairs = [keep.tile([P, T, 2], BF16, name="pairs%d" % u, align_bytes=64) for u in range(2)]
 
@@ -151,39 +156,45 @@ def tile_moe_sup_lin_relu2_kernel(tc, x_words, x_scales, w1, w2_words, w2_scales
             else:
                 nc.scalar.activation(out=dst, in_=src, func=ACT.Square)
 
-        apart = [keep.tile([P, 2, HALF], F32, name="apart0")]
-        woven = [keep.tile([P, HALF, 2], F32, name="woven0", tag="relu")]
+        apart = keep.tile([P, 2, T], F32, name="apart", tag="relu")
 
-        def relu_early(u):
-            for a, b in early_pieces[2 * u]:
-                for e in range(2):
-                    relu(u == 0 and e == 1, apart[u][:, e, a:b], early_sums[2 * u + e, a][:])
+        def relu_quarter(q):
+            a, b = quarters[q]
+            for t in range(2):
+                relu(t == 1, apart[:, t, a:b], sums[t, q][:])
 
-        def relu_late(u, c):
-            relu(u == 0, woven[u][:, QUARTER * c : QUARTER * (c + 1), :], late_sums[u, c][:].rearrange("p e n -> p n e"))
+        def square_quarter(q):
+            a, b = quarters[q]
+            cut = a + VECTOR_SQUARES[q]
+            for on_vector, c, d in ((True, a, cut), (False, cut, b)):
+                square(on_vector, pairs[0][:, c:d, :], apart[:, :, c:d].rearrange("p e n -> p n e"))
 
-        def square_early(u, a, b):
-            square(False, pairs[u][:, a:b, :], apart[u][:, :, a:b].rearrange("p e n -> p n e"))
-
-        def square_late(on_vector, u, a, b):
-            square(on_vector, pairs[u][:, HALF + a : HALF + b, :], woven[u][:, a:b, :])
-
-        relu_early(0)
-        square_early(0, 0, QUARTER)
-        relu_late(0, 0)
-        square_early(0, QUARTER, HALF)
-        relu_late(0, 1)
-        square_late(False, 0, 0, QUARTER)
-        square_late(True, 0, QUARTER, QUARTER + VECTOR_SQUARES)
-        square_late(False, 0, QUARTER + VECTOR_SQUARES, HALF)
+        for t in range(2):
+            late_group(t, sums[t, 2][:], 2)
+        relu_quarter(0)
+        for t in range(2):
+            late_group(t, sums[t, 3][:], 3)
+        for t in (2, 3):
+            first_layer(1, t, early_sums[t][:], 0, HALF, False)
+        relu_quarter(1)
+        for c in range(2):
+            for e in range(2):
+                late_group(2 + e, late_sums[c][:, e, :], 2 + c)
+        square_quarter(0)
+        relu_quarter(2)
+        square_quarter(1)
+        relu_quarter(3)
+        square_quarter(2)
+        square_quarter(3)
         second = keep.tile([P, 2, T], F32, name="second", tag="relu")
-        apart.append(second[:, 0, :].rearrange("p (e n) -> p e n", e=2))
-        woven.append(second[:, 1, :].rearrange("p (n e) -> p n e", e=2))
-        relu_early(1)
-        relu_late(1, 0)
-        relu_late(1, 1)
-        square_early(1, 0, HALF)
-        square_late(False, 1, 0, HALF)
+        early = second[:, 0, :].rearrange("p (e n) -> p e n", e=2)
+        late = second[:, 1, :].rearrange("p (n e) -> p n e", e=2)
+        for e in range(2):
+            relu(False, early[:, e, :], early_sums[2 + e][:])
+        for c in range(2):
+            relu(False, late[:, QUARTER * c : QUARTER * (c + 1), :], late_sums[c][:].rearrange("p e n -> p n e"))
+        square(False, pairs[1][:, 0:HALF, :], early.rearrange("p e n -> p n e"))
+        square(False, pairs[1][:, HALF:T, :], late)
 
         windows = [pairs[u][:].rearrange("p n e -> p (n e)").bitcast(U32) for u in range(2)]
         picked = keep.tile([P, S // AHEAD + 1, AHEAD], U32, name="picked", tag="picked", align_bytes=64)
@@ -211,6 +222,7 @@ def tile_moe_sup_lin_relu2_kernel(tc, x_words, x_scales, w1, w2_words, w2_scales
 
         for a, b in spans(FIRST_PAIR_CUTS):
             gather_pairs(0, a, b)
+
         chunks = [(S - b, S - a) for a, b in spans(SLOT_CHUNKS)]
         tail = len(chunks) - LAG
         held = {}

@@ -27,8 +27,8 @@ FIRST_PAIR_CUTS = (768, 768, 512)
 SLOT_CHUNKS = (256,) * 7 + (128, 128)
 LAG = 4
 AHEAD = 1024
-TOKEN_PIECES = ((384, 384, 256), (384, 448, 128, 64))
-PSUM_PIECES = 4
+SHARED_PIECES = ((384, 384), (256, 256, 128))
+SHARED = [sum(widths) for widths in SHARED_PIECES]
 
 
 def spans(widths):
@@ -88,7 +88,11 @@ def tile_moe_sup_lin_relu2_kernel(tc, x_words, x_scales, w1, w2_words, w2_scales
         nc.sync.dma_start(back_lists[0][:], pos1)
         nc.sync.dma_start(back_lists[1][:], pos2)
         gates = keep.tile([P, 2, T], F32, name="gates", align_bytes=64)
-        nc.sync.dma_start(out=gates[:], in_=gate.rearrange("r p t -> p r t"))
+        nc.sync.dma_start(out=gates[:, 0, :], in_=gate[0])
+        nc.sync.dma_start(out=gates[:, 1, min(SHARED) : T], in_=gate[1, :, min(SHARED) : T])
+        gate_cols = keep.tile([P, max(SHARED) // P], F32, name="gate_cols")
+        with nc.allow_non_contiguous_dma(reason="one gate a partition"):
+            nc.sync.dma_start(out=gate_cols[:], in_=gate[1, 0, 0 : max(SHARED)].rearrange("(c p) -> p c", p=P))
 
         w1_codes, w1_plane = {}, {}
 
@@ -265,40 +269,60 @@ def tile_moe_sup_lin_relu2_kernel(tc, x_words, x_scales, w1, w2_words, w2_scales
 
         identity = keep.tile([P, P], F32, name="identity")
         make_identity(nc, identity[:])
-        pieces = [(rows, a, b) for rows in range(2) for a, b in spans(TOKEN_PIECES[rows])]
-        terms = {}
+        pieces = [(rows, a, b) for rows in range(2) for a, b in spans(SHARED_PIECES[rows])]
+        lead = pieces[0][2]
+        first_lead = keep.tile([P, lead], F32, name="first_lead", tag="lead")
+        first = keep.tile([P, 2, T], F32, name="first")
+        plain, backs = {}, {}
 
-        def fetch(r, rows, a, b):
-            terms[rows, a, r] = keep.tile([P, b - a], F32, name="term%d_%d_%d" % (rows, a, r))
-            nc.vector.tensor_tensor(out=terms[rows, a, r][:], in0=y[rows][:].indirect(back_lists[r][:, a // 16 : b // 16]),
-                                    in1=gates[:, r, a:b], op=ALU.mult)
+        def fetch(r, rows, a, b, dst):
+            nc.vector.tensor_tensor(out=dst, in0=y[rows][:].indirect(back_lists[r][:, a // 16 : b // 16]), in1=gates[:, r, a:b], op=ALU.mult)
 
-        def combine(rows, a, b):
+        def fetch_plain(g):
+            rows, a, b = pieces[g]
+            plain[g] = keep.tile([P, b - a], F32, name="plain%d" % g, tag="plain%d" % (g % 2))
+            nc.scalar.activation(out=plain[g][:], in_=y[rows][:].indirect(back_lists[1][:, a // 16 : b // 16]), func=ACT.Copy)
+
+        def gate_turned(g):
+            rows, a, b = pieces[g]
+            blocks = spans((P,) * ((b - a) // P))
+            turned = psum.tile([P, b - a], F32, name="turned%d" % g, tag="bank%d" % (1 + g % 2))
+            for c, d in blocks:
+                nc.tensor.transpose(turned[:, c:d], plain[g][:, c:d], identity[:])
+            scaled = keep.tile([P, b - a], F32, name="scaled%d" % g)
+            for c, d in blocks:
+                col = (a + c) // P
+                nc.scalar.activation(out=scaled[:, c:d], in_=turned[:, c:d], func=ACT.Copy, scale=gate_cols[:, col : col + 1])
+            backs[g] = psum.tile([P, b - a], F32, name="back%d" % g, tag="bank%d" % (3 + g))
+            for c, d in blocks:
+                nc.tensor.transpose(backs[g][:, c:d], scaled[:, c:d], identity[:])
+
+        def add_and_store(rows, a, b, one, other):
             res = keep.tile([P, b - a], F32, name="res%d_%d" % (rows, a))
-            nc.vector.tensor_tensor(out=res[:], in0=terms[rows, a, 0][:], in1=terms[rows, a, 1][:], op=ALU.add)
+            nc.vector.tensor_tensor(out=res[:], in0=one, in1=other, op=ALU.add)
             nc.sync.dma_start(out=out[P * rows : P * (rows + 1), a:b], in_=res[:])
 
-        def combine_in_psum(i, rows, a, b):
-            blocks = spans((P,) * ((b - a) // P))
-            turned = psum.tile([P, b - a], F32, name="turned%d" % i, tag="bank%d" % (i % 2))
-            for c, d in blocks:
-                for r in range(2):
-                    nc.tensor.matmul(turned[:, c:d], lhsT=terms[rows, a, r][:, c:d], rhs=identity[:],
-                                     start=(r == 0), stop=(r == 1), is_transpose=True)
-            summed = keep.tile([P, b - a], F32, name="summed%d" % i)
-            nc.scalar.copy(out=summed[:], in_=turned[:])
-            back = psum.tile([P, b - a], F32, name="back%d" % i, tag="bank%d" % (2 + i % 2))
-            for c, d in blocks:
-                nc.tensor.transpose(back[:, c:d], summed[:, c:d], identity[:])
-            res = keep.tile([P, b - a], F32, name="res%d_%d" % (rows, a))
-            nc.scalar.copy(out=res[:], in_=back[:])
-            nc.scalar.dma_start(out=out[P * rows : P * (rows + 1), a:b], in_=res[:])
+        def add_shared(g):
+            rows, a, b = pieces[g]
+            add_and_store(rows, a, b, backs[g][:], first_lead[:] if g == 0 else first[:, rows, a:b])
 
-        for i, piece in enumerate(pieces):
-            fetch(0, *piece)
-            fetch(1, *piece)
-            if i < PSUM_PIECES:
-                combine_in_psum(i, *piece)
-            elif i > PSUM_PIECES:
-                combine(*pieces[i - 1])
-        combine(*pieces[-1])
+        fetch_plain(0)
+        fetch_plain(1)
+        for g in range(len(pieces)):
+            gate_turned(g)
+            if g + 2 < len(pieces):
+                fetch_plain(g + 2)
+        own0 = keep.tile([P, T - SHARED[0]], F32, name="own0")
+        fetch(1, 0, SHARED[0], T, own0[:])
+        fetch(0, 0, lead, T, first[:, 0, lead:T])
+        fetch(0, 0, 0, lead, first_lead[:])
+        add_and_store(0, SHARED[0], T, first[:, 0, SHARED[0] : T], own0[:])
+        fetch(0, 1, 0, HALF, first[:, 1, 0:HALF])
+        fetch(0, 1, HALF, T, first[:, 1, HALF:T])
+        add_shared(0)
+        own1 = keep.tile([P, T - SHARED[1]], F32, name="own1", tag="lead")
+        fetch(1, 1, SHARED[1], T, own1[:])
+        add_shared(1)
+        add_and_store(1, SHARED[1], T, first[:, 1, SHARED[1] : T], own1[:])
+        for g in range(2, len(pieces)):
+            add_shared(g)

@@ -27,7 +27,7 @@ FIRST_PAIR_CUTS = (768, 768, 512)
 SLOT_CHUNKS = (256,) * 7 + (128, 128)
 LAG = 4
 AHEAD = 1024
-SHARED_PIECES = ((384, 384), (256, 256, 128))
+SHARED_PIECES = ((384, 512), (256, 256, 128))
 SHARED = [sum(widths) for widths in SHARED_PIECES]
 
 

@@ -27,7 +27,7 @@ FIRST_PAIR_CUTS = (768, 768, 512)
 SLOT_CHUNKS = (256,) * 7 + (128, 128)
 LAG = 4
 AHEAD = 1024
-SHARED_PIECES = ((384, 512), (256, 256, 128))
+SHARED_PIECES = ((384, 384, 256), (256, 256, 128))
 SHARED = [sum(widths) for widths in SHARED_PIECES]
 
 
@@ -293,7 +293,7 @@ def tile_moe_sup_lin_relu2_kernel(tc, x_words, x_scales, w1, w2_words, w2_scales
             for c, d in blocks:
                 col = (a + c) // P
                 nc.scalar.activation(out=scaled[:, c:d], in_=turned[:, c:d], func=ACT.Copy, scale=gate_cols[:, col : col + 1])
-            backs[g] = psum.tile([P, b - a], F32, name="back%d" % g, tag="bank%d" % (3 + g))
+            backs[g] = psum.tile([P, b - a], F32, name="back%d" % g, tag="bank%d" % ((3 + g) % BANKS))
             for c, d in blocks:
                 nc.tensor.transpose(backs[g][:, c:d], scaled[:, c:d], identity[:])
 
@@ -312,11 +312,8 @@ def tile_moe_sup_lin_relu2_kernel(tc, x_words, x_scales, w1, w2_words, w2_scales
             gate_turned(g)
             if g + 2 < len(pieces):
                 fetch_plain(g + 2)
-        own0 = keep.tile([P, T - SHARED[0]], F32, name="own0")
-        fetch(1, 0, SHARED[0], T, own0[:])
         fetch(0, 0, lead, T, first[:, 0, lead:T])
         fetch(0, 0, 0, lead, first_lead[:])
-        add_and_store(0, SHARED[0], T, first[:, 0, SHARED[0] : T], own0[:])
         fetch(0, 1, 0, HALF, first[:, 1, 0:HALF])
         fetch(0, 1, HALF, T, first[:, 1, HALF:T])
         add_shared(0)

@@ -270,9 +270,8 @@ def tile_moe_sup_lin_relu2_kernel(tc, x_words, x_scales, w1, w2_words, w2_scales
         identity = keep.tile([P, P], F32, name="identity")
         make_identity(nc, identity[:])
         pieces = [(rows, a, b) for rows in range(2) for a, b in spans(SHARED_PIECES[rows])]
-        lead = pieces[0][2]
-        first_lead = keep.tile([P, lead], F32, name="first_lead", tag="lead")
-        first = keep.tile([P, 2, T], F32, name="first")
+        row0 = len(SHARED_PIECES[0])
+        first0 = keep.tile([P, T], F32, name="first0")
         plain, backs = {}, {}
 
         def fetch(r, rows, a, b, dst):
@@ -289,7 +288,7 @@ def tile_moe_sup_lin_relu2_kernel(tc, x_words, x_scales, w1, w2_words, w2_scales
             turned = psum.tile([P, b - a], F32, name="turned%d" % g, tag="bank%d" % (1 + g % 2))
             for c, d in blocks:
                 nc.tensor.transpose(turned[:, c:d], plain[g][:, c:d], identity[:])
-            scaled = keep.tile([P, b - a], F32, name="scaled%d" % g)
+            scaled = keep.tile([P, b - a], F32, name="scaled%d" % g, tag="spent%d" % g)
             for c, d in blocks:
                 col = (a + c) // P
                 nc.scalar.activation(out=scaled[:, c:d], in_=turned[:, c:d], func=ACT.Copy, scale=gate_cols[:, col : col + 1])
@@ -302,24 +301,25 @@ def tile_moe_sup_lin_relu2_kernel(tc, x_words, x_scales, w1, w2_words, w2_scales
             nc.vector.tensor_tensor(out=res[:], in0=one, in1=other, op=ALU.add)
             nc.sync.dma_start(out=out[P * rows : P * (rows + 1), a:b], in_=res[:])
 
-        def add_shared(g):
-            rows, a, b = pieces[g]
-            add_and_store(rows, a, b, backs[g][:], first_lead[:] if g == 0 else first[:, rows, a:b])
-
         fetch_plain(0)
         fetch_plain(1)
         for g in range(len(pieces)):
             gate_turned(g)
             if g + 2 < len(pieces):
                 fetch_plain(g + 2)
-        fetch(0, 0, lead, T, first[:, 0, lead:T])
-        fetch(0, 0, 0, lead, first_lead[:])
-        fetch(0, 1, 0, HALF, first[:, 1, 0:HALF])
-        fetch(0, 1, HALF, T, first[:, 1, HALF:T])
-        add_shared(0)
-        own1 = keep.tile([P, T - SHARED[1]], F32, name="own1", tag="lead")
-        fetch(1, 1, SHARED[1], T, own1[:])
-        add_shared(1)
-        add_and_store(1, SHARED[1], T, first[:, 1, SHARED[1] : T], own1[:])
-        for g in range(2, len(pieces)):
-            add_shared(g)
+        fetch(0, 0, 0, HALF, first0[:, 0:HALF])
+        fetch(0, 0, HALF, T, first0[:, HALF:T])
+        own = [keep.tile([P, T - SHARED[1]], F32, name="own%d" % r) for r in range(2)]
+        for r in range(2):
+            fetch(r, 1, SHARED[1], T, own[r][:])
+        add_and_store(1, SHARED[1], T, own[0][:], own[1][:])
+        first1 = {}
+        for g in range(row0):
+            rows, a, b = pieces[g]
+            add_and_store(rows, a, b, backs[g][:], first0[:, a:b])
+            rows, a, b = pieces[row0 + g]
+            first1[g] = keep.tile([P, b - a], F32, name="first1_%d" % g, tag="spent%d" % g)
+            fetch(0, rows, a, b, first1[g][:])
+        for g in range(row0):
+            rows, a, b = pieces[row0 + g]
+            add_and_store(rows, a, b, backs[row0 + g][:], first1[g][:])

@@ -23,11 +23,11 @@ BANKS = 8
 HALF = T // 2
 QUARTER = T // 4
 VECTOR_SQUARES = (112, 112, 112, 96)
-FIRST_PAIR_CUTS = (768, 768, 512)
-SLOT_CHUNKS = (256,) * 7 + (128, 128)
-LAG = 4
-AHEAD = 1024
-SHARED_PIECES = ((384, 384, 256), (256, 256, 128))
+CHUNK = 256
+ROW = (1, 5, 8, 0, 4, 7, 0, 3)
+PLACE = (1, 4, 6, 0, 3, 5, 7, 2)
+GPSIMD_SQUARES = (256, 256, 0, 0)
+SHARED_PIECES = ((384, 384, 256), (256, 256, 256))
 SHARED = [sum(widths) for widths in SHARED_PIECES]
 
 
@@ -114,11 +114,10 @@ def tile_moe_sup_lin_relu2_kernel(tc, x_words, x_scales, w1, w2_words, w2_scales
 
         sums = {(t, q): psum.tile([P, QUARTER], F32, name="sums%d_%d" % (t, q), tag="bank%d" % ((0, 2, 6, 0)[q] + t))
                 for q in range(4) for t in range(2)}
-        early_sums = {t: psum.tile([P, HALF], F32, name="early_sums%d" % t, tag="bank%d" % (t + 2)) for t in (2, 3)}
-        late_sums = [psum.tile([P, 2, QUARTER], F32, name="late_sums%d" % c, tag="bank%d" % (2 + c)) for c in range(2)]
+        woven = [psum.tile([P, 2, QUARTER], F32, name="woven%d" % q, tag="bank%d" % (4, 5, 2, 3)[q]) for q in range(4)]
         quarters = spans((QUARTER,) * 4)
 
-        def first_layer(s, t, acc, a, b, opens):
+        def first_layer(s, t, acc, a, b, opens, closes):
             cols = slice(P * (t % 2), P * (t % 2 + 1))
             words = x_early[s][:, 4 * a : 4 * b] if a < HALF else x_late[(a - HALF) // QUARTER][:, s, :]
             nc.tensor.matmul_mx(
@@ -128,23 +127,24 @@ def tile_moe_sup_lin_relu2_kernel(tc, x_words, x_scales, w1, w2_words, w2_scales
                 rhs=words.bitcast(FP8X4),
                 rhs_scale=x_plane[4 * s : P, a:b],
                 start=opens,
-                stop=not opens,
+                stop=closes,
             )
 
         quantise_w1(0)
         for t in range(2):
             for q in range(2):
-                first_layer(0, t, sums[t, q][:], *quarters[q], True)
-        for t in (2, 3):
-            first_layer(0, t, early_sums[t][:], 0, HALF, True)
+                first_layer(0, t, sums[t, q][:], *quarters[q], True, False)
+        for e in range(2):
+            for q in range(2):
+                first_layer(0, 2 + e, woven[q][:, e, :], *quarters[q], e == 0, False)
         quantise_w1(1)
         for q in range(2):
             for t in range(2):
-                first_layer(1, t, sums[t, q][:], *quarters[q], False)
+                first_layer(1, t, sums[t, q][:], *quarters[q], False, True)
 
         def late_group(t, acc, q):
             for s in (1, 0):
-                first_layer(s, t, acc, *quarters[q], s == 1)
+                first_layer(s, t, acc, *quarters[q], s == 1, s == 0)
 
         pairs = [keep.tile([P, T, 2], BF16, name="pairs%d" % u, align_bytes=64) for u in range(2)]
 
@@ -178,39 +178,37 @@ def tile_moe_sup_lin_relu2_kernel(tc, x_words, x_scales, w1, w2_words, w2_scales
         relu_quarter(0)
         for t in range(2):
             late_group(t, sums[t, 3][:], 3)
-        for t in (2, 3):
-            first_layer(1, t, early_sums[t][:], 0, HALF, False)
+        for q in range(2):
+            for e in range(2):
+                first_layer(1, 2 + e, woven[q][:, e, :], *quarters[q], False, e == 1)
         relu_quarter(1)
         for c in range(2):
             for e in range(2):
-                late_group(2 + e, late_sums[c][:, e, :], 2 + c)
+                late_group(2 + e, woven[2 + c][:, e, :], 2 + c)
         square_quarter(0)
         relu_quarter(2)
         square_quarter(1)
         relu_quarter(3)
         square_quarter(2)
         square_quarter(3)
-        second = keep.tile([P, 2, T], F32, name="second", tag="relu")
-        early = second[:, 0, :].rearrange("p (e n) -> p e n", e=2)
-        late = second[:, 1, :].rearrange("p (n e) -> p n e", e=2)
-        for e in range(2):
-            relu(False, early[:, e, :], early_sums[2 + e][:])
-        for c in range(2):
-            relu(False, late[:, QUARTER * c : QUARTER * (c + 1), :], late_sums[c][:].rearrange("p e n -> p n e"))
-        square(False, pairs[1][:, 0:HALF, :], early.rearrange("p e n -> p n e"))
-        square(False, pairs[1][:, HALF:T, :], late)
+        second = keep.tile([P, T, 2], F32, name="second", tag="relu")
+        for q, (a, b) in enumerate(quarters):
+            relu(False, second[:, a:b, :], woven[q][:].rearrange("p e n -> p n e"))
+            cut = a + GPSIMD_SQUARES[q]
+            if cut > a:
+                nc.gpsimd.tensor_tensor(out=pairs[1][:, a:cut, :], in0=second[:, a:cut, :], in1=second[:, a:cut, :], op=ALU.mult)
+        rest = sum(GPSIMD_SQUARES)
+        square(False, pairs[1][:, rest:T, :], second[:, rest:T, :])
 
         windows = [pairs[u][:].rearrange("p n e -> p (n e)").bitcast(U32) for u in range(2)]
-        picked = keep.tile([P, S // AHEAD + 1, AHEAD], U32, name="picked", tag="picked", align_bytes=64)
-        picked_run = picked[:].rearrange("p r n -> p (r n)")
-        slots = keep.tile([P, S, 4], BF16, name="slots", align_bytes=64)
-        slot_words = slots[:].bitcast(U32)
-        h_codes = keep.tile([P, S], U32, name="h_codes", align_bytes=64)
+        picked = keep.tile([P, 10, CHUNK], U32, name="picked", tag="picked", align_bytes=64)
+        slots, h_codes = {}, {}
         h_plane = keep.tile([P, S], U8, name="h_plane", align_bytes=64)
-        y = [keep.tile([P, S], F32, name="y0")]
+        y = [keep.tile([P, S], F32, name="y%d" % rows, align_bytes=64) for rows in range(2)]
 
-        def gather_pairs(u, a, b):
-            nc.vector.tensor_copy(out=picked_run[:, AHEAD * u + a : AHEAD * u + b], in_=windows[u].indirect(slot_list[:, a // 16 : b // 16]))
+        def gather_pairs(u, row, a, b):
+            dst = picked[:].rearrange("p r n -> p (r n)")[:, CHUNK * row : CHUNK * row + b - a]
+            nc.vector.tensor_copy(out=dst, in_=windows[u].indirect(slot_list[:, a // 16 : b // 16]))
 
         def second_layer(rows, a, b, acc):
             for e in range(a // C, b // C):
@@ -218,52 +216,77 @@ def tile_moe_sup_lin_relu2_kernel(tc, x_words, x_scales, w1, w2_words, w2_scales
                     out=acc[:, C * e - a : C * (e + 1) - a],
                     lhsT=w2_codes[:, e, 2 * P * rows : 2 * P * (rows + 1)].bitcast(FP4X4),
                     lhsT_scale=w2_plane[:, e, P * rows : P * (rows + 1)],
-                    rhs=h_codes[:, C * e : C * (e + 1)].bitcast(FP8X4),
+                    rhs=h_codes[e].bitcast(FP8X4),
                     rhs_scale=h_plane[:, C * e : C * (e + 1)],
                     start=True,
                     stop=True,
                 )
 
-        for a, b in spans(FIRST_PAIR_CUTS):
-            gather_pairs(0, a, b)
+        def span(i):
+            a = CHUNK * PLACE[min(i, 7)] + (C if i == 8 else 0)
+            return a, a + (CHUNK if i < 7 else C)
 
-        chunks = [(S - b, S - a) for a, b in spans(SLOT_CHUNKS)]
-        tail = len(chunks) - LAG
-        held = {}
+        accs = {}
+
+        def fetch_chunk(i):
+            a = CHUNK * PLACE[i]
+            if i == 6:
+                gather_pairs(0, ROW[i], a, a + CHUNK)
+            gather_pairs(1, ROW[i] + 1, a, a + CHUNK)
+
+        def interleave(i):
+            a, b = span(i)
+            row = ROW[min(i, 7)]
+            both = picked[:, row : row + 2, a % CHUNK : a % CHUNK + b - a]
+            if i > 6:
+                c, d = span(13 - i)
+                slots[i] = y[0][:, c:d].bitcast(U32)
+            else:
+                tag = "codes%d" % (i - 4) if i >= 4 else "slots%d" % i
+                slots[i] = keep.tile([P, 2 * (b - a)], U32, name="slots%d" % i, tag=tag, align_bytes=64)[:]
+            nc.scalar.copy(out=slots[i].rearrange("p (n u) -> p n u", u=2), in_=both.rearrange("p u n -> p n u"))
 
         def quantise_slots(i):
-            a, b = chunks[i]
-            nc.vector.quantize_mx(
-                out=h_codes[:, a:b].bitcast(FP8X4),
-                scales=h_plane[:, a:b],
-                in_=slots[:, a:b, :].rearrange("p n t -> p (n t)"),
-            )
+            a, b = span(i)
+            codes = keep.tile([P, b - a], U32, name="h_codes%d" % i, tag="codes%d" % i, align_bytes=64)
+            for e in range(a // C, b // C):
+                h_codes[e] = codes[:, C * e - a : C * (e + 1) - a]
+            nc.vector.quantize_mx(out=codes[:].bitcast(FP8X4), scales=h_plane[:, a:b], in_=slots[i].bitcast(BF16))
             acc = psum.tile([P, 2, b - a], F32, name="acc%d" % i, tag="bank%d" % (i % BANKS))
             second_layer(0, a, b, acc[:, 0, :])
-            if 0 < i < tail:
+            accs[0, i] = acc[:, 0, :]
+            if i < 5:
                 second_layer(1, a, b, acc[:, 1, :])
-                held[i] = acc
-            if i >= tail:
-                nc.vector.tensor_copy(out=y[0][:, a:b], in_=acc[:, 0, :])
+                accs[1, i] = acc[:, 1, :]
+
+        def empty(rows, i, on_vector=False):
+            a, b = span(i)
+            if on_vector:
+                nc.vector.tensor_copy(out=y[rows][:, a:b], in_=accs[rows, i])
             else:
-                nc.scalar.copy(out=y[0][:, a:b], in_=acc[:, 0, :])
+                nc.scalar.copy(out=y[rows][:, a:b], in_=accs[rows, i])
 
-        for i, (a, b) in enumerate(chunks):
-            if i >= LAG:
-                quantise_slots(i - LAG)
-            gather_pairs(1, a, b)
-            both = picked[:, a // AHEAD : a // AHEAD + 2, a % AHEAD : a % AHEAD + b - a]
-            nc.scalar.copy(out=slot_words[:, a:b, :], in_=both.rearrange("p u n -> p n u"))
-        for i in range(tail, len(chunks)):
+        gather_pairs(0, 0, 0, 2 * CHUNK)
+        gather_pairs(0, 3, 2 * CHUNK, 5 * CHUNK)
+        gather_pairs(0, 7, 5 * CHUNK, 7 * CHUNK)
+        for i in range(3):
+            fetch_chunk(i)
+        for i in range(9):
+            interleave(i)
             quantise_slots(i)
-
-        y.append(keep.tile([P, S], F32, name="y1", tag="picked", align_bytes=64))
-        for i, acc in held.items():
-            a, b = chunks[i]
-            nc.scalar.copy(out=y[1][:, a:b], in_=acc[:, 1, :])
-        left = [(tail, chunks[tail]), (tail + 1, chunks[tail + 1]), (tail + 2, (0, 2 * C)), (tail + 3, chunks[0])]
-        for i, (a, b) in left:
-            acc = psum.tile([P, b - a], F32, name="left_acc%d" % i, tag="bank%d" % (i % BANKS))
+            if i < 5:
+                fetch_chunk(i + 3)
+            if 3 <= i < 7:
+                empty(0, i - 3)
+            if 3 <= i < 5:
+                empty(1, i - 3)
+        empty(0, 4)
+        for i in (6, 5, 7, 8):
+            empty(0, i, True)
+        for i in range(2, 5):
+            empty(1, i)
+        for bank, (a, b) in ((1, span(5)), (2, span(6)), (3, (span(7)[0], span(8)[1]))):
+            acc = psum.tile([P, b - a], F32, name="left_acc%d" % bank, tag="bank%d" % bank)
             second_layer(1, a, b, acc)
             nc.scalar.copy(out=y[1][:, a:b], in_=acc[:])
 
@@ -285,14 +308,14 @@ def tile_moe_sup_lin_relu2_kernel(tc, x_words, x_scales, w1, w2_words, w2_scales
         def gate_turned(g):
             rows, a, b = pieces[g]
             blocks = spans((P,) * ((b - a) // P))
-            turned = psum.tile([P, b - a], F32, name="turned%d" % g, tag="bank%d" % (1 + g % 2))
+            turned = psum.tile([P, b - a], F32, name="turned%d" % g, tag="bank%d" % (4 + g % 2))
             for c, d in blocks:
                 nc.tensor.transpose(turned[:, c:d], plain[g][:, c:d], identity[:])
             scaled = keep.tile([P, b - a], F32, name="scaled%d" % g, tag="spent%d" % g)
             for c, d in blocks:
                 col = (a + c) // P
                 nc.scalar.activation(out=scaled[:, c:d], in_=turned[:, c:d], func=ACT.Copy, scale=gate_cols[:, col : col + 1])
-            backs[g] = psum.tile([P, b - a], F32, name="back%d" % g, tag="bank%d" % ((3 + g) % BANKS))
+            backs[g] = psum.tile([P, b - a], F32, name="back%d" % g, tag="bank%d" % (6, 7, 0, 1, 2, 3)[g])
             for c, d in blocks:
                 nc.tensor.transpose(backs[g][:, c:d], scaled[:, c:d], identity[:])
 

@@ -25,9 +25,9 @@ QUARTER = T // 4
 VECTOR_SQUARES = (112, 112, 112, 96)
 CHUNK = 256
 ROW = (1, 5, 8, 0, 4, 7, 0, 3)
-PLACE = (1, 4, 6, 0, 3, 5, 7, 2)
+PLACE = (1, 4, 7, 0, 3, 6, 5, 2)
 GPSIMD_SQUARES = (256, 256, 0, 0)
-SHARED_PIECES = ((384, 384, 256), (256, 256, 256))
+SHARED_PIECES = ((384, 384, 256), (384, 384, 128))
 SHARED = [sum(widths) for widths in SHARED_PIECES]
 
 
@@ -238,11 +238,11 @@ def tile_moe_sup_lin_relu2_kernel(tc, x_words, x_scales, w1, w2_words, w2_scales
             a, b = span(i)
             row = ROW[min(i, 7)]
             both = picked[:, row : row + 2, a % CHUNK : a % CHUNK + b - a]
-            if i > 6:
-                c, d = span(13 - i)
-                slots[i] = y[0][:, c:d].bitcast(U32)
+            if i == 8:
+                border = span(5)[0]
+                slots[i] = y[0][:, border - C : border + C].bitcast(U32)
             else:
-                tag = "codes%d" % (i - 4) if i >= 4 else "slots%d" % i
+                tag = "codes%d" % (i - 4) if 4 <= i < 7 else "slots%d" % i
                 slots[i] = keep.tile([P, 2 * (b - a)], U32, name="slots%d" % i, tag=tag, align_bytes=64)[:]
             nc.scalar.copy(out=slots[i].rearrange("p (n u) -> p n u", u=2), in_=both.rearrange("p u n -> p n u"))
 
@@ -268,7 +268,7 @@ def tile_moe_sup_lin_relu2_kernel(tc, x_words, x_scales, w1, w2_words, w2_scales
 
         gather_pairs(0, 0, 0, 2 * CHUNK)
         gather_pairs(0, 3, 2 * CHUNK, 5 * CHUNK)
-        gather_pairs(0, 7, 5 * CHUNK, 7 * CHUNK)
+        gather_pairs(0, 7, 6 * CHUNK, 8 * CHUNK)
         for i in range(3):
             fetch_chunk(i)
         for i in range(9):
@@ -278,12 +278,12 @@ def tile_moe_sup_lin_relu2_kernel(tc, x_words, x_scales, w1, w2_words, w2_scales
                 fetch_chunk(i + 3)
             if 3 <= i < 7:
                 empty(0, i - 3)
-            if 3 <= i < 5:
+            if 3 <= i < 6:
                 empty(1, i - 3)
         empty(0, 4)
-        for i in (6, 5, 7, 8):
+        for i in range(5, 9):
             empty(0, i, True)
-        for i in range(2, 5):
+        for i in range(3, 5):
             empty(1, i)
         for bank, (a, b) in ((1, span(5)), (2, span(6)), (3, (span(7)[0], span(8)[1]))):
             acc = psum.tile([P, b - a], F32, name="left_acc%d" % bank, tag="bank%d" % bank)

@@ -24,10 +24,10 @@ HALF = T // 2
 QUARTER = T // 4
 VECTOR_SQUARES = (112, 112, 112, 96)
 CHUNK = 256
-ROW = (1, 5, 8, 0, 4, 7, 0, 3)
-PLACE = (1, 4, 7, 0, 3, 6, 5, 2)
+ROW = (1, 2, 4, 0, 1, 3, 0, 0)
+PLACE = (4, 7, 2, 3, 6, 1, 0, 5)
 GPSIMD_SQUARES = (256, 256, 0, 0)
-SHARED_PIECES = ((384, 384, 256), (384, 384, 128))
+SHARED_PIECES = ((384, 384, 256), (256, 256, 128))
 SHARED = [sum(widths) for widths in SHARED_PIECES]
 
 
@@ -198,17 +198,20 @@ def tile_moe_sup_lin_relu2_kernel(tc, x_words, x_scales, w1, w2_words, w2_scales
             if cut > a:
                 nc.gpsimd.tensor_tensor(out=pairs[1][:, a:cut, :], in0=second[:, a:cut, :], in1=second[:, a:cut, :], op=ALU.mult)
         rest = sum(GPSIMD_SQUARES)
-        square(False, pairs[1][:, rest:T, :], second[:, rest:T, :])
+        for a, b in ((rest, T - QUARTER), (T - QUARTER, T)):
+            square(False, pairs[1][:, a:b, :], second[:, a:b, :])
 
         windows = [pairs[u][:].rearrange("p n e -> p (n e)").bitcast(U32) for u in range(2)]
-        picked = keep.tile([P, 10, CHUNK], U32, name="picked", tag="picked", align_bytes=64)
+        picked = keep.tile([P, 6 * CHUNK], U32, name="picked", align_bytes=64)
         slots, h_codes = {}, {}
         h_plane = keep.tile([P, S], U8, name="h_plane", align_bytes=64)
         y = [keep.tile([P, S], F32, name="y%d" % rows, align_bytes=64) for rows in range(2)]
 
-        def gather_pairs(u, row, a, b):
-            dst = picked[:].rearrange("p r n -> p (r n)")[:, CHUNK * row : CHUNK * row + b - a]
-            nc.vector.tensor_copy(out=dst, in_=windows[u].indirect(slot_list[:, a // 16 : b // 16]))
+        homes = [y[0][:].bitcast(U32) if i % 3 == 1 else picked[:] for i in range(8)]
+
+        def gather_pairs(u, i, a, b):
+            row = ROW[i] + u
+            nc.vector.tensor_copy(out=homes[i][:, CHUNK * row : CHUNK * row + b - a], in_=windows[u].indirect(slot_list[:, a // 16 : b // 16]))
 
         def second_layer(rows, a, b, acc):
             for e in range(a // C, b // C):
@@ -231,19 +234,16 @@ def tile_moe_sup_lin_relu2_kernel(tc, x_words, x_scales, w1, w2_words, w2_scales
         def fetch_chunk(i):
             a = CHUNK * PLACE[i]
             if i == 6:
-                gather_pairs(0, ROW[i], a, a + CHUNK)
-            gather_pairs(1, ROW[i] + 1, a, a + CHUNK)
+                gather_pairs(0, i, a, a + CHUNK)
+            gather_pairs(1, i, a, a + CHUNK)
 
         def interleave(i):
             a, b = span(i)
             row = ROW[min(i, 7)]
-            both = picked[:, row : row + 2, a % CHUNK : a % CHUNK + b - a]
-            if i == 8:
-                border = span(5)[0]
-                slots[i] = y[0][:, border - C : border + C].bitcast(U32)
-            else:
-                tag = "codes%d" % (i - 4) if 4 <= i < 7 else "slots%d" % i
-                slots[i] = keep.tile([P, 2 * (b - a)], U32, name="slots%d" % i, tag=tag, align_bytes=64)[:]
+            rows = homes[min(i, 7)][:, CHUNK * row : CHUNK * (row + 2)].rearrange("p (u n) -> p u n", u=2)
+            both = rows[:, :, a % CHUNK : a % CHUNK + b - a]
+            tag = "codes%d" % (i - 4) if 4 <= i < 7 else "slots%d" % i
+            slots[i] = keep.tile([P, 2 * (b - a)], U32, name="slots%d" % i, tag=tag, align_bytes=64)[:]
             nc.scalar.copy(out=slots[i].rearrange("p (n u) -> p n u", u=2), in_=both.rearrange("p u n -> p n u"))
 
         def quantise_slots(i):
@@ -255,7 +255,7 @@ def tile_moe_sup_lin_relu2_kernel(tc, x_words, x_scales, w1, w2_words, w2_scales
             acc = psum.tile([P, 2, b - a], F32, name="acc%d" % i, tag="bank%d" % (i % BANKS))
             second_layer(0, a, b, acc[:, 0, :])
             accs[0, i] = acc[:, 0, :]
-            if i < 5:
+            if i not in (5, 6):
                 second_layer(1, a, b, acc[:, 1, :])
                 accs[1, i] = acc[:, 1, :]
 
@@ -266,9 +266,9 @@ def tile_moe_sup_lin_relu2_kernel(tc, x_words, x_scales, w1, w2_words, w2_scales
             else:
                 nc.scalar.copy(out=y[rows][:, a:b], in_=accs[rows, i])
 
-        gather_pairs(0, 0, 0, 2 * CHUNK)
-        gather_pairs(0, 3, 2 * CHUNK, 5 * CHUNK)
-        gather_pairs(0, 7, 6 * CHUNK, 8 * CHUNK)
+        gather_pairs(0, 3, 3 * CHUNK, 5 * CHUNK)
+        gather_pairs(0, 7, 5 * CHUNK, 8 * CHUNK)
+        gather_pairs(0, 5, CHUNK, 3 * CHUNK)
         for i in range(3):
             fetch_chunk(i)
         for i in range(9):
@@ -280,12 +280,14 @@ def tile_moe_sup_lin_relu2_kernel(tc, x_words, x_scales, w1, w2_words, w2_scales
                 empty(0, i - 3)
             if 3 <= i < 6:
                 empty(1, i - 3)
-        empty(0, 4)
-        for i in range(5, 9):
-            empty(0, i, True)
+        for i in range(4, 7):
+            empty(0, i, i > 5)
+        for i in (7, 8):
+            for rows in range(2):
+                empty(rows, i, True)
         for i in range(3, 5):
             empty(1, i)
-        for bank, (a, b) in ((1, span(5)), (2, span(6)), (3, (span(7)[0], span(8)[1]))):
+        for bank, (a, b) in ((1, span(5)), (2, span(6))):
             acc = psum.tile([P, b - a], F32, name="left_acc%d" % bank, tag="bank%d" % bank)
             second_layer(1, a, b, acc)
             nc.scalar.copy(out=y[1][:, a:b], in_=acc[:])
@@ -335,14 +337,16 @@ def tile_moe_sup_lin_relu2_kernel(tc, x_words, x_scales, w1, w2_words, w2_scales
         own = [keep.tile([P, T - SHARED[1]], F32, name="own%d" % r) for r in range(2)]
         for r in range(2):
             fetch(r, 1, SHARED[1], T, own[r][:])
-        add_and_store(1, SHARED[1], T, own[0][:], own[1][:])
         first1 = {}
-        for g in range(row0):
+
+        def fetch_first1(g, tag):
             rows, a, b = pieces[g]
-            add_and_store(rows, a, b, backs[g][:], first0[:, a:b])
-            rows, a, b = pieces[row0 + g]
-            first1[g] = keep.tile([P, b - a], F32, name="first1_%d" % g, tag="spent%d" % g)
+            first1[g] = keep.tile([P, b - a], F32, name="first1_%d" % g, tag=tag)
             fetch(0, rows, a, b, first1[g][:])
-        for g in range(row0):
-            rows, a, b = pieces[row0 + g]
-            add_and_store(rows, a, b, backs[row0 + g][:], first1[g][:])
+
+        fetch_first1(row0, "first1")
+        add_and_store(1, SHARED[1], T, own[0][:], own[1][:])
+        for g, (rows, a, b) in enumerate(pieces):
+            add_and_store(rows, a, b, backs[g][:], first1[g][:] if rows else first0[:, a:b])
+            if row0 + 1 + g < len(pieces):
+                fetch_first1(row0 + 1 + g, "spent%d" % g)

@@ -27,7 +27,7 @@ CHUNK = 256
 ROW = (1, 2, 4, 0, 1, 3, 0, 0)
 PLACE = (4, 7, 2, 3, 6, 1, 0, 5)
 GPSIMD_SQUARES = (256, 256, 0, 0)
-SHARED_PIECES = ((384, 384, 256), (256, 256, 128))
+SHARED_PIECES = ((384, 384, 256), (384, 256, 128))
 SHARED = [sum(widths) for widths in SHARED_PIECES]
 
 

@@ -22,7 +22,7 @@ P = 128
 BANKS = 8
 HALF = T // 2
 QUARTER = T // 4
-VECTOR_SQUARES = (112, 112, 112, 96)
+VECTOR_SQUARES = (112, 112, 112)
 CHUNK = 256
 ROW = (1, 2, 4, 0, 1, 3, 0, 0)
 PLACE = (4, 7, 2, 3, 6, 1, 0, 5)
@@ -99,27 +99,28 @@ def tile_moe_sup_lin_relu2_kernel(tc, x_words, x_scales, w1, w2_words, w2_scales
         def quantise_w1(s):
             grouped = [keep.tile([P, 2, P, 4], BF16, name="w1_grouped%d%d" % (s, u), align_bytes=64) for u in range(2)]
             by_lane = w1_raw[s][:].rearrange("p j (m t) -> p m t j", t=4)
+            halves = spans((P // 2, P // 2))
             for a, b in row_pairs:
-                nc.vector.tensor_copy(out=grouped[0][:].rearrange("p e m j -> p m e j")[:, :, :, a:b], in_=by_lane[:, :, 0:2, a:b])
+                for c, d in halves:
+                    nc.vector.tensor_copy(out=grouped[0][:].rearrange("p e m j -> p m e j")[:, c:d, :, a:b], in_=by_lane[:, c:d, 0:2, a:b])
                 nc.scalar.activation(out=grouped[1][:].rearrange("p e m j -> p m e j")[:, :, :, a:b], in_=by_lane[:, :, 2:4, a:b], func=ACT.Copy)
             for u in range(2):
                 w1_codes[s, u] = keep.tile([P, 2 * P], U32, name="w1_codes%d%d" % (s, u), align_bytes=64)
                 w1_plane[s, u] = keep.tile([P, 2 * P], U8, name="w1_plane%d%d" % (s, u), align_bytes=64)
-                for a, b in spans((1, 1) if u == 0 else (2,)):
-                    nc.vector.quantize_mx(
-                        out=w1_codes[s, u][:, P * a : P * b].bitcast(FP8X4),
-                        scales=w1_plane[s, u][:, P * a : P * b],
-                        in_=grouped[u][:, a:b].rearrange("p e m j -> p (e m j)"),
-                    )
+                flat = grouped[u][:].rearrange("p e m j -> p (e m j)")
+                parts = [(P * e + c, P * e + d) for c, d in halves for e in range(2)] if u == 0 else [(0, 2 * P)]
+                for a, b in parts:
+                    nc.vector.quantize_mx(out=w1_codes[s, u][:, a:b].bitcast(FP8X4), scales=w1_plane[s, u][:, a:b], in_=flat[:, 4 * a : 4 * b])
 
         sums = {(t, q): psum.tile([P, QUARTER], F32, name="sums%d_%d" % (t, q), tag="bank%d" % ((0, 2, 6, 0)[q] + t))
-                for q in range(4) for t in range(2)}
-        woven = [psum.tile([P, 2, QUARTER], F32, name="woven%d" % q, tag="bank%d" % (4, 5, 2, 3)[q]) for q in range(4)]
+                for q in range(3) for t in range(2)}
+        last_sums = [psum.tile([P, 2, P], F32, name="last_sums%d" % c, tag="bank%d" % c) for c in range(2)]
+        woven = [psum.tile([P, 2, QUARTER], F32, name="woven%d" % q, tag="bank%d" % (4, 5, 0, 1)[q]) for q in range(4)]
         quarters = spans((QUARTER,) * 4)
 
         def first_layer(s, t, acc, a, b, opens, closes):
             cols = slice(P * (t % 2), P * (t % 2 + 1))
-            words = x_early[s][:, 4 * a : 4 * b] if a < HALF else x_late[(a - HALF) // QUARTER][:, s, :]
+            words = x_early[s][:, 4 * a : 4 * b] if a < HALF else x_late[(a - HALF) // QUARTER][:, s, 4 * (a % QUARTER) : 4 * (a % QUARTER + b - a)]
             nc.tensor.matmul_mx(
                 out=acc,
                 lhsT=w1_codes[s, t // 2][:, cols].bitcast(FP8X4),
@@ -142,9 +143,9 @@ def tile_moe_sup_lin_relu2_kernel(tc, x_words, x_scales, w1, w2_words, w2_scales
             for t in range(2):
                 first_layer(1, t, sums[t, q][:], *quarters[q], False, True)
 
-        def late_group(t, acc, q):
+        def late_group(t, acc, a, b):
             for s in (1, 0):
-                first_layer(s, t, acc, *quarters[q], s == 1, s == 0)
+                first_layer(s, t, acc, a, b, s == 1, s == 0)
 
         pairs = [keep.tile([P, T, 2], BF16, name="pairs%d" % u, align_bytes=64) for u in range(2)]
 
@@ -174,23 +175,28 @@ def tile_moe_sup_lin_relu2_kernel(tc, x_words, x_scales, w1, w2_words, w2_scales
                 square(on_vector, pairs[0][:, c:d, :], apart[:, :, c:d].rearrange("p e n -> p n e"))
 
         for t in range(2):
-            late_group(t, sums[t, 2][:], 2)
+            late_group(t, sums[t, 2][:], *quarters[2])
         relu_quarter(0)
-        for t in range(2):
-            late_group(t, sums[t, 3][:], 3)
+        steps = [(T - QUARTER + a, T - QUARTER + b) for a, b in spans((P, P))]
+        for c in range(2):
+            for t in range(2):
+                late_group(t, last_sums[c][:, t, :], *steps[c])
         for q in range(2):
             for e in range(2):
                 first_layer(1, 2 + e, woven[q][:, e, :], *quarters[q], False, e == 1)
         relu_quarter(1)
-        for c in range(2):
-            for e in range(2):
-                late_group(2 + e, woven[2 + c][:, e, :], 2 + c)
         square_quarter(0)
         relu_quarter(2)
         square_quarter(1)
-        relu_quarter(3)
         square_quarter(2)
-        square_quarter(3)
+        last = [apart[:, c, T - QUARTER : T].rearrange("p (n e) -> p n e", e=2) for c in range(2)]
+        for c in range(2):
+            relu(c == 1, last[c], last_sums[c][:].rearrange("p e n -> p n e"))
+        for c in range(2):
+            for e in range(2):
+                late_group(2 + e, woven[2 + c][:, e, :], *quarters[2 + c])
+        for c, (a, b) in enumerate(steps):
+            square(c == 0, pairs[0][:, a:b, :], last[c])
         second = keep.tile([P, T, 2], F32, name="second", tag="relu")
         for q, (a, b) in enumerate(quarters):
             relu(False, second[:, a:b, :], woven[q][:].rearrange("p e n -> p n e"))

@@ -264,6 +264,10 @@ def tile_moe_sup_lin_relu2_kernel(tc, x_words, x_scales, w1, w2_words, w2_scales
             if i not in (5, 6):
                 second_layer(1, a, b, acc[:, 1, :])
                 accs[1, i] = acc[:, 1, :]
+            if i == 3:
+                idle = psum.tile([P, 2, b - a], F32, name="idle", tag="bank0")
+                for rows in range(2):
+                    second_layer(rows, a, b, idle[:, rows, :])
 
         def empty(rows, i, on_vector=False):
             a, b = span(i)

@@ -27,8 +27,8 @@ CHUNK = 256
 ROW = (1, 2, 4, 0, 1, 3, 0, 0)
 PLACE = (4, 7, 2, 3, 6, 1, 0, 5)
 GPSIMD_SQUARES = (256, 256, 0, 0)
+OWN = 256
 SHARED_PIECES = ((384, 384, 256), (384, 256, 128))
-SHARED = [sum(widths) for widths in SHARED_PIECES]
 
 
 def spans(widths):
@@ -89,10 +89,10 @@ def tile_moe_sup_lin_relu2_kernel(tc, x_words, x_scales, w1, w2_words, w2_scales
         nc.sync.dma_start(back_lists[1][:], pos2)
         gates = keep.tile([P, 2, T], F32, name="gates", align_bytes=64)
         nc.sync.dma_start(out=gates[:, 0, :], in_=gate[0])
-        nc.sync.dma_start(out=gates[:, 1, min(SHARED) : T], in_=gate[1, :, min(SHARED) : T])
-        gate_cols = keep.tile([P, max(SHARED) // P], F32, name="gate_cols")
+        nc.sync.dma_start(out=gates[:, 1, 0:OWN], in_=gate[1, :, 0:OWN])
+        gate_cols = keep.tile([P, T // P], F32, name="gate_cols")
         with nc.allow_non_contiguous_dma(reason="one gate a partition"):
-            nc.sync.dma_start(out=gate_cols[:], in_=gate[1, 0, 0 : max(SHARED)].rearrange("(c p) -> p c", p=P))
+            nc.sync.dma_start(out=gate_cols[:], in_=gate[1, 0, :].rearrange("(c p) -> p c", p=P))
 
         w1_codes, w1_plane = {}, {}
 
@@ -261,7 +261,7 @@ def tile_moe_sup_lin_relu2_kernel(tc, x_words, x_scales, w1, w2_words, w2_scales
             acc = psum.tile([P, 2, b - a], F32, name="acc%d" % i, tag="bank%d" % (i % BANKS))
             second_layer(0, a, b, acc[:, 0, :])
             accs[0, i] = acc[:, 0, :]
-            if i not in (5, 6):
+            if i < 5 or i == 8:
                 second_layer(1, a, b, acc[:, 1, :])
                 accs[1, i] = acc[:, 1, :]
             if i == 3:
@@ -290,21 +290,19 @@ def tile_moe_sup_lin_relu2_kernel(tc, x_words, x_scales, w1, w2_words, w2_scales
                 empty(0, i - 3)
             if 3 <= i < 6:
                 empty(1, i - 3)
-        for i in range(4, 7):
+        for i in range(4, 9):
             empty(0, i, i > 5)
-        for i in (7, 8):
-            for rows in range(2):
-                empty(rows, i, True)
+        empty(1, 8, True)
         for i in range(3, 5):
             empty(1, i)
-        for bank, (a, b) in ((1, span(5)), (2, span(6))):
+        for bank, (a, b) in ((1, (span(6)[0], span(5)[1])), (2, span(7))):
             acc = psum.tile([P, b - a], F32, name="left_acc%d" % bank, tag="bank%d" % bank)
             second_layer(1, a, b, acc)
             nc.scalar.copy(out=y[1][:, a:b], in_=acc[:])
 
         identity = keep.tile([P, P], F32, name="identity")
         make_identity(nc, identity[:])
-        pieces = [(rows, a, b) for rows in range(2) for a, b in spans(SHARED_PIECES[rows])]
+        pieces = [(rows, OWN * rows + a, OWN * rows + b) for rows in range(2) for a, b in spans(SHARED_PIECES[rows])]
         row0 = len(SHARED_PIECES[0])
         first0 = keep.tile([P, T], F32, name="first0")
         plain, backs = {}, {}
@@ -331,8 +329,8 @@ def tile_moe_sup_lin_relu2_kernel(tc, x_words, x_scales, w1, w2_words, w2_scales
             for c, d in blocks:
                 nc.tensor.transpose(backs[g][:, c:d], scaled[:, c:d], identity[:])
 
-        def add_and_store(rows, a, b, one, other):
-            res = keep.tile([P, b - a], F32, name="res%d_%d" % (rows, a))
+        def add_and_store(rows, a, b, one, other, tag):
+            res = keep.tile([P, b - a], F32, name="res%d_%d" % (rows, a), tag=tag)
             nc.vector.tensor_tensor(out=res[:], in0=one, in1=other, op=ALU.add)
             nc.sync.dma_start(out=out[P * rows : P * (rows + 1), a:b], in_=res[:])
 
@@ -342,21 +340,19 @@ def tile_moe_sup_lin_relu2_kernel(tc, x_words, x_scales, w1, w2_words, w2_scales
             gate_turned(g)
             if g + 2 < len(pieces):
                 fetch_plain(g + 2)
-        fetch(0, 0, 0, HALF, first0[:, 0:HALF])
-        fetch(0, 0, HALF, T, first0[:, HALF:T])
-        own = [keep.tile([P, T - SHARED[1]], F32, name="own%d" % r) for r in range(2)]
-        for r in range(2):
-            fetch(r, 1, SHARED[1], T, own[r][:])
-        first1 = {}
-
-        def fetch_first1(g, tag):
-            rows, a, b = pieces[g]
-            first1[g] = keep.tile([P, b - a], F32, name="first1_%d" % g, tag=tag)
-            fetch(0, rows, a, b, first1[g][:])
-
-        fetch_first1(row0, "first1")
-        add_and_store(1, SHARED[1], T, own[0][:], own[1][:])
+        fetch(0, 0, 0, T, first0[:])
+        lead = pieces[row0][2]
+        first_lead = keep.tile([P, lead], F32, name="first_lead")
+        fetch(0, 1, 0, lead, first_lead[:])
+        own = keep.tile([P, OWN], F32, name="own")
+        fetch(1, 1, 0, OWN, own[:])
+        first = {g: first0[:, a:b] for g, (rows, a, b) in enumerate(pieces[:row0])}
+        first[row0] = first_lead[:, OWN:lead]
         for g, (rows, a, b) in enumerate(pieces):
-            add_and_store(rows, a, b, backs[g][:], first1[g][:] if rows else first0[:, a:b])
-            if row0 + 1 + g < len(pieces):
-                fetch_first1(row0 + 1 + g, "spent%d" % g)
+            add_and_store(rows, a, b, backs[g][:], first[g], "sum%d" % g)
+            if g == 0:
+                add_and_store(1, 0, OWN, first_lead[:, 0:OWN], own[:], "spent0")
+            elif g < row0:
+                rows, a, b = pieces[row0 + g]
+                first[row0 + g] = keep.tile([P, b - a], F32, name="first1_%d" % g, tag="spent%d" % g)[:]
+                fetch(0, rows, a, b, first[row0 + g])

from contextlib import ExitStack

import concourse.mybir as mybir
from concourse.masks import make_identity

K, T, E, C, H, N = 1024, 1024, 16, 128, 512, 256
S = E * C
FLOPS = 2 * K * H * T + 2 * H * N * S

F32 = mybir.dt.float32
BF16 = mybir.dt.bfloat16
I32 = mybir.dt.int32
U32 = mybir.dt.uint32
U16 = mybir.dt.uint16
U8 = mybir.dt.uint8
FP8X4 = mybir.dt.float8_e4m3fn_x4
FP4X4 = mybir.dt.float4_e2m1fn_x4
ACT = mybir.ActivationFunctionType
ALU = mybir.AluOpType

P = 128
BANKS = 8
HALF = T // 2
QUARTER = T // 4
VECTOR_SQUARES = (112, 112, 112)
CHUNK = 256
ROW = (1, 2, 4, 0, 1, 3, 0, 0)
PLACE = (4, 7, 2, 3, 6, 1, 0, 5)
GPSIMD_SQUARES = (256, 256, 0, 0)
OWN = 256
SHARED_PIECES = ((384, 384, 256), (384, 256, 128))


def spans(widths):
    cuts, start = [], 0
    for width in widths:
        cuts.append((start, start + width))
        start += width
    return cuts


def tile_moe_sup_lin_relu2_kernel(tc, x_words, x_scales, w1, w2_words, w2_scales, gate, offs, pos1, pos2, out):
    nc = tc.nc
    with ExitStack() as ctx:
        lists = ctx.enter_context(tc.tile_pool(name="lists", bufs=1))
        keep = ctx.enter_context(tc.tile_pool(name="keep", bufs=1))
        psum = ctx.enter_context(tc.psum_pool(name="psum", bufs=1))

        x_plane = keep.tile([P, T], U8, name="x_plane", align_bytes=64)
        nc.vector.memset(x_plane[:].bitcast(I32), 0)
        w2_plane = keep.tile([P, E, N], U8, name="w2_plane", align_bytes=64)
        nc.vector.memset(w2_plane[:].bitcast(I32), 0)

        w1_raw = [keep.tile([P, 4, H], F32, name="w1_raw%d" % s, align_bytes=64) for s in range(2)]
        x_early = [keep.tile([P, 4 * HALF], U8, name="x_early%d" % s, align_bytes=64) for s in range(2)]
        x_late = [keep.tile([P, 2, 4 * QUARTER], U8, name="x_late%d" % c, align_bytes=64) for c in range(2)]
        x_rows = x_words.rearrange("s p t d -> s p (t d)")
        w1_rows = w1.rearrange("(s p j) c -> s p j c", s=2, j=4)
        row_pairs = spans((2, 2))

        def load_w1(s):
            for a, b in row_pairs:
                nc.sync.dma_start(out=w1_raw[s][:, a:b, :], in_=w1_rows[s, :, a:b, :])

        def load_early(s):
            nc.sync.dma_start(out=x_early[s][:].bitcast(I32), in_=x_rows[s, :, 0 : 4 * HALF].bitcast(I32))

        def load_late(c):
            a = 4 * (HALF + QUARTER * c)
            nc.sync.dma_start(out=x_late[c][:].bitcast(I32), in_=x_rows[:, :, a : a + 4 * QUARTER].rearrange("s p b -> p s b").bitcast(I32))

        load_w1(0)
        for q in range(4):
            nc.scalar.dma_start(out=x_plane[32 * q : 32 * q + 8, :].bitcast(I32), in_=x_scales[:, 4 * q : 4 * q + 4, :].bitcast(I32))
        load_early(0)
        load_w1(1)
        load_early(1)
        load_late(0)
        load_late(1)
        slot_list = lists.tile([P, S // 16], U16, name="slot_list")
        nc.sync.dma_start(slot_list[:], offs)
        w2_scale_rows = w2_scales.rearrange("e s (q r) n -> r q (e s) n", r=4)
        for r in range(4):
            nc.sync.dma_start(out=w2_plane[r:P:32, :, :].bitcast(I32), in_=w2_scale_rows[r].bitcast(I32))
        w2_codes = keep.tile([P, E, 2 * N], U8, name="w2_codes", align_bytes=64)
        nc.sync.dma_start(out=w2_codes[:].bitcast(I32), in_=w2_words.rearrange("e s p b -> p (e s) b").bitcast(I32))
        back_lists = [lists.tile([P, T // 16], U16, name="back_list%d" % r) for r in range(2)]
        nc.sync.dma_start(back_lists[0][:], pos1)
        nc.sync.dma_start(back_lists[1][:], pos2)
        gates = keep.tile([P, 2, T], F32, name="gates", align_bytes=64)
        nc.sync.dma_start(out=gates[:, 0, :], in_=gate[0])
        nc.sync.dma_start(out=gates[:, 1, 0:OWN], in_=gate[1, :, 0:OWN])
        gate_cols = keep.tile([P, T // P], F32, name="gate_cols")
        with nc.allow_non_contiguous_dma(reason="one gate a partition"):
            nc.sync.dma_start(out=gate_cols[:], in_=gate[1, 0, :].rearrange("(c p) -> p c", p=P))

        w1_codes, w1_plane = {}, {}

        def quantise_w1(s):
            grouped = [keep.tile([P, 2, P, 4], BF16, name="w1_grouped%d%d" % (s, u), align_bytes=64) for u in range(2)]
            by_lane = w1_raw[s][:].rearrange("p j (m t) -> p m t j", t=4)
            halves = spans((P // 2, P // 2))
            for a, b in row_pairs:
                for c, d in halves:
                    nc.vector.tensor_copy(out=grouped[0][:].rearrange("p e m j -> p m e j")[:, c:d, :, a:b], in_=by_lane[:, c:d, 0:2, a:b])
                nc.scalar.activation(out=grouped[1][:].rearrange("p e m j -> p m e j")[:, :, :, a:b], in_=by_lane[:, :, 2:4, a:b], func=ACT.Copy)
            for u in range(2):
                w1_codes[s, u] = keep.tile([P, 2 * P], U32, name="w1_codes%d%d" % (s, u), align_bytes=64)
                w1_plane[s, u] = keep.tile([P, 2 * P], U8, name="w1_plane%d%d" % (s, u), align_bytes=64)
                flat = grouped[u][:].rearrange("p e m j -> p (e m j)")
                parts = [(P * e + c, P * e + d) for c, d in halves for e in range(2)] if u == 0 else [(0, 2 * P)]
                for a, b in parts:
                    nc.vector.quantize_mx(out=w1_codes[s, u][:, a:b].bitcast(FP8X4), scales=w1_plane[s, u][:, a:b], in_=flat[:, 4 * a : 4 * b])

        sums = {(t, q): psum.tile([P, QUARTER], F32, name="sums%d_%d" % (t, q), tag="bank%d" % ((0, 2, 6, 0)[q] + t))
                for q in range(3) for t in range(2)}
        last_sums = [psum.tile([P, 2, P], F32, name="last_sums%d" % c, tag="bank%d" % c) for c in range(2)]
        woven = [psum.tile([P, 2, QUARTER], F32, name="woven%d" % q, tag="bank%d" % (4, 5, 0, 1)[q]) for q in range(4)]
        quarters = spans((QUARTER,) * 4)

        def first_layer(s, t, acc, a, b, opens, closes):
            cols = slice(P * (t % 2), P * (t % 2 + 1))
            words = x_early[s][:, 4 * a : 4 * b] if a < HALF else x_late[(a - HALF) // QUARTER][:, s, 4 * (a % QUARTER) : 4 * (a % QUARTER + b - a)]
            nc.tensor.matmul_mx(
                out=acc,
                lhsT=w1_codes[s, t // 2][:, cols].bitcast(FP8X4),
                lhsT_scale=w1_plane[s, t // 2][:, cols],
                rhs=words.bitcast(FP8X4),
                rhs_scale=x_plane[4 * s : P, a:b],
                start=opens,
                stop=closes,
            )

        quantise_w1(0)
        for t in range(2):
            for q in range(2):
                first_layer(0, t, sums[t, q][:], *quarters[q], True, False)
        for e in range(2):
            for q in range(2):
                first_layer(0, 2 + e, woven[q][:, e, :], *quarters[q], e == 0, False)
        quantise_w1(1)
        for q in range(2):
            for t in range(2):
                first_layer(1, t, sums[t, q][:], *quarters[q], False, True)

        def late_group(t, acc, a, b):
            for s in (1, 0):
                first_layer(s, t, acc, a, b, s == 1, s == 0)

        pairs = [keep.tile([P, T, 2], BF16, name="pairs%d" % u, align_bytes=64) for u in range(2)]

        def relu(on_vector, dst, src):
            if on_vector:
                nc.vector.tensor_scalar_max(out=dst, in0=src, scalar1=0.0)
            else:
                nc.scalar.activation(out=dst, in_=src, func=ACT.Relu)

        def square(on_vector, dst, src):
            if on_vector:
                nc.vector.tensor_tensor(out=dst, in0=src, in1=src, op=ALU.mult)
            else:
                nc.scalar.activation(out=dst, in_=src, func=ACT.Square)

        apart = keep.tile([P, 2, T], F32, name="apart", tag="relu")

        def relu_quarter(q):
            a, b = quarters[q]
            for t in range(2):
                relu(t == 1, apart[:, t, a:b], sums[t, q][:])

        def square_quarter(q):
            a, b = quarters[q]
            cut = a + VECTOR_SQUARES[q]
            for on_vector, c, d in ((True, a, cut), (False, cut, b)):
                square(on_vector, pairs[0][:, c:d, :], apart[:, :, c:d].rearrange("p e n -> p n e"))

        for t in range(2):
            late_group(t, sums[t, 2][:], *quarters[2])
        relu_quarter(0)
        steps = [(T - QUARTER + a, T - QUARTER + b) for a, b in spans((P, P))]
        for c in range(2):
            for t in range(2):
                late_group(t, last_sums[c][:, t, :], *steps[c])
        for q in range(2):
            for e in range(2):
                first_layer(1, 2 + e, woven[q][:, e, :], *quarters[q], False, e == 1)
        relu_quarter(1)
        square_quarter(0)
        relu_quarter(2)
        square_quarter(1)
        square_quarter(2)
        last = [apart[:, c, T - QUARTER : T].rearrange("p (n e) -> p n e", e=2) for c in range(2)]
        for c in range(2):
            relu(c == 1, last[c], last_sums[c][:].rearrange("p e n -> p n e"))
        for c in range(2):
            for e in range(2):
                late_group(2 + e, woven[2 + c][:, e, :], *quarters[2 + c])
        for c, (a, b) in enumerate(steps):
            square(c == 0, pairs[0][:, a:b, :], last[c])
        second = keep.tile([P, T, 2], F32, name="second", tag="relu")
        for q, (a, b) in enumerate(quarters):
            relu(False, second[:, a:b, :], woven[q][:].rearrange("p e n -> p n e"))
            cut = a + GPSIMD_SQUARES[q]
            if cut > a:
                nc.gpsimd.tensor_tensor(out=pairs[1][:, a:cut, :], in0=second[:, a:cut, :], in1=second[:, a:cut, :], op=ALU.mult)
        rest = sum(GPSIMD_SQUARES)
        for a, b in ((rest, T - QUARTER), (T - QUARTER, T)):
            square(False, pairs[1][:, a:b, :], second[:, a:b, :])

        windows = [pairs[u][:].rearrange("p n e -> p (n e)").bitcast(U32) for u in range(2)]
        picked = keep.tile([P, 6 * CHUNK], U32, name="picked", align_bytes=64)
        slots, h_codes = {}, {}
        h_plane = keep.tile([P, S], U8, name="h_plane", align_bytes=64)
        y = [keep.tile([P, S], F32, name="y%d" % rows, align_bytes=64) for rows in range(2)]

        homes = [y[0][:].bitcast(U32) if i % 3 == 1 else picked[:] for i in range(8)]

        def gather_pairs(u, i, a, b):
            row = ROW[i] + u
            nc.vector.tensor_copy(out=homes[i][:, CHUNK * row : CHUNK * row + b - a], in_=windows[u].indirect(slot_list[:, a // 16 : b // 16]))

        def second_layer(rows, a, b, acc):
            for e in range(a // C, b // C):
                nc.tensor.matmul_mx(
                    out=acc[:, C * e - a : C * (e + 1) - a],
                    lhsT=w2_codes[:, e, 2 * P * rows : 2 * P * (rows + 1)].bitcast(FP4X4),
                    lhsT_scale=w2_plane[:, e, P * rows : P * (rows + 1)],
                    rhs=h_codes[e].bitcast(FP8X4),
                    rhs_scale=h_plane[:, C * e : C * (e + 1)],
                    start=True,
                    stop=True,
                )

        def span(i):
            a = CHUNK * PLACE[min(i, 7)] + (C if i == 8 else 0)
            return a, a + (CHUNK if i < 7 else C)

        accs = {}

        def fetch_chunk(i):
            a = CHUNK * PLACE[i]
            if i == 6:
                gather_pairs(0, i, a, a + CHUNK)
            gather_pairs(1, i, a, a + CHUNK)

        def interleave(i):
            a, b = span(i)
            row = ROW[min(i, 7)]
            rows = homes[min(i, 7)][:, CHUNK * row : CHUNK * (row + 2)].rearrange("p (u n) -> p u n", u=2)
            both = rows[:, :, a % CHUNK : a % CHUNK + b - a]
            tag = "codes%d" % (i - 4) if 4 <= i < 7 else "slots%d" % i
            slots[i] = keep.tile([P, 2 * (b - a)], U32, name="slots%d" % i, tag=tag, align_bytes=64)[:]
            nc.scalar.copy(out=slots[i].rearrange("p (n u) -> p n u", u=2), in_=both.rearrange("p u n -> p n u"))

        def quantise_slots(i):
            a, b = span(i)
            codes = keep.tile([P, b - a], U32, name="h_codes%d" % i, tag="codes%d" % i, align_bytes=64)
            for e in range(a // C, b // C):
                h_codes[e] = codes[:, C * e - a : C * (e + 1) - a]
            nc.vector.quantize_mx(out=codes[:].bitcast(FP8X4), scales=h_plane[:, a:b], in_=slots[i].bitcast(BF16))
            acc = psum.tile([P, 2, b - a], F32, name="acc%d" % i, tag="bank%d" % (i % BANKS))
            second_layer(0, a, b, acc[:, 0, :])
            accs[0, i] = acc[:, 0, :]
            if i < 5 or i == 8:
                second_layer(1, a, b, acc[:, 1, :])
                accs[1, i] = acc[:, 1, :]
            if i == 3:
                idle = psum.tile([P, 2, b - a], F32, name="idle", tag="bank0")
                for rows in range(2):
                    second_layer(rows, a, b, idle[:, rows, :])

        def empty(rows, i, on_vector=False):
            a, b = span(i)
            if on_vector:
                nc.vector.tensor_copy(out=y[rows][:, a:b], in_=accs[rows, i])
            else:
                nc.scalar.copy(out=y[rows][:, a:b], in_=accs[rows, i])

        gather_pairs(0, 3, 3 * CHUNK, 5 * CHUNK)
        gather_pairs(0, 7, 5 * CHUNK, 8 * CHUNK)
        gather_pairs(0, 5, CHUNK, 3 * CHUNK)
        for i in range(3):
            fetch_chunk(i)
        for i in range(9):
            interleave(i)
            quantise_slots(i)
            if i < 5:
                fetch_chunk(i + 3)
            if 3 <= i < 7:
                empty(0, i - 3)
            if 3 <= i < 6:
                empty(1, i - 3)
        for i in range(4, 9):
            empty(0, i, i > 5)
        empty(1, 8, True)
        for i in range(3, 5):
            empty(1, i)
        for bank, (a, b) in ((1, (span(6)[0], span(5)[1])), (2, span(7))):
            acc = psum.tile([P, b - a], F32, name="left_acc%d" % bank, tag="bank%d" % bank)
            second_layer(1, a, b, acc)
            nc.scalar.copy(out=y[1][:, a:b], in_=acc[:])

        identity = keep.tile([P, P], F32, name="identity")
        make_identity(nc, identity[:])
        pieces = [(rows, OWN * rows + a, OWN * rows + b) for rows in range(2) for a, b in spans(SHARED_PIECES[rows])]
        row0 = len(SHARED_PIECES[0])
        first0 = keep.tile([P, T], F32, name="first0")
        plain, backs = {}, {}

        def fetch(r, rows, a, b, dst):
            nc.vector.tensor_tensor(out=dst, in0=y[rows][:].indirect(back_lists[r][:, a // 16 : b // 16]), in1=gates[:, r, a:b], op=ALU.mult)

        def fetch_plain(g):
            rows, a, b = pieces[g]
            plain[g] = keep.tile([P, b - a], F32, name="plain%d" % g, tag="plain%d" % (g % 2))
            nc.scalar.activation(out=plain[g][:], in_=y[rows][:].indirect(back_lists[1][:, a // 16 : b // 16]), func=ACT.Copy)

        def gate_turned(g):
            rows, a, b = pieces[g]
            blocks = spans((P,) * ((b - a) // P))
            turned = psum.tile([P, b - a], F32, name="turned%d" % g, tag="bank%d" % (4 + g % 2))
            for c, d in blocks:
                nc.tensor.transpose(turned[:, c:d], plain[g][:, c:d], identity[:])
            scaled = keep.tile([P, b - a], F32, name="scaled%d" % g, tag="spent%d" % g)
            for c, d in blocks:
                col = (a + c) // P
                nc.scalar.activation(out=scaled[:, c:d], in_=turned[:, c:d], func=ACT.Copy, scale=gate_cols[:, col : col + 1])
            backs[g] = psum.tile([P, b - a], F32, name="back%d" % g, tag="bank%d" % (6, 7, 0, 1, 2, 3)[g])
            for c, d in blocks:
                nc.tensor.transpose(backs[g][:, c:d], scaled[:, c:d], identity[:])

        def add_and_store(rows, a, b, one, other, tag):
            res = keep.tile([P, b - a], F32, name="res%d_%d" % (rows, a), tag=tag)
            nc.vector.tensor_tensor(out=res[:], in0=one, in1=other, op=ALU.add)
            nc.sync.dma_start(out=out[P * rows : P * (rows + 1), a:b], in_=res[:])

        fetch_plain(0)
        fetch_plain(1)
        for g in range(len(pieces)):
            gate_turned(g)
            if g + 2 < len(pieces):
                fetch_plain(g + 2)
        fetch(0, 0, 0, T, first0[:])
        lead = pieces[row0][2]
        first_lead = keep.tile([P, lead], F32, name="first_lead")
        fetch(0, 1, 0, lead, first_lead[:])
        own = keep.tile([P, OWN], F32, name="own")
        fetch(1, 1, 0, OWN, own[:])
        first = {g: first0[:, a:b] for g, (rows, a, b) in enumerate(pieces[:row0])}
        first[row0] = first_lead[:, OWN:lead]
        for g, (rows, a, b) in enumerate(pieces):
            add_and_store(rows, a, b, backs[g][:], first[g], "sum%d" % g)
            if g == 0:
                add_and_store(1, 0, OWN, first_lead[:, 0:OWN], own[:], "spent0")
            elif g < row0:
                rows, a, b = pieces[row0 + g]
                first[row0 + g] = keep.tile([P, b - a], F32, name="first1_%d" % g, tag="spent%d" % g)[:]
                fetch(0, rows, a, b, first[row0 + g])
